import numpy as np, ml_dtypes
CORES = [5,29,101,125,133,157,229,253]
N = 8
import mx_ref
BF = ml_dtypes.bfloat16
def gcols(t, e):
    v = np.concatenate([t.reshape(8, 16, -1, 4), np.zeros((8, 16, 1, 4), BF)], axis=2)
    return np.ascontiguousarray(np.stack([v[g][:, e[g]] for g in range(8)])).reshape(128, -1)
def cut(t, i, w=512):
    return t[:, w * i:w * i + w]
def pick(q, e):
    c = np.concatenate([q[0].reshape(128, -1, 4), np.zeros((128, 1, 4), np.uint8)], axis=1); s = np.concatenate([q[1], np.ones((16, 1), np.uint8)], axis=1)
    return (np.ascontiguousarray(c[:, e].reshape(128, -1)), np.ascontiguousarray(s[:, e]))
def join(*qs):
    return (np.concatenate([q[0] for q in qs], axis=1), np.concatenate([q[1] for q in qs], axis=1))
def put(q, e, v):
    c, s = q[0].reshape(128, -1, 4).copy(), q[1].copy(); c[:, e] = v[0].reshape(128, -1, 4); s[:, e] = v[1]
    return (c.reshape(128, -1), s)
def pk(c, s):
    return (np.ascontiguousarray(c), mx_ref.live(s))
def emit(q):
    return q[0], q[1]
def packed(v, rng):
    q = [mx_ref.quantize(np.ascontiguousarray(v[r])) for r in range(N)]
    return np.stack([a for a, b in q]), np.stack([mx_ref.plane(b, rng) for a, b in q])
def values_of_codes():
    e, c = np.zeros((128, 128, 4), np.float32), np.zeros((128, 2, 4), np.uint8)
    e[np.arange(128), np.arange(128), 0] = 1
    c[:127, :, 0] = np.arange(256).reshape(2, 128).T[:127]
    return mx_ref.matmul(mx_ref.quantize(e.reshape(128, 512).astype(BF)), (c.reshape(128, 8), np.full((16, 2), 127, np.uint8))).T.reshape(-1).astype(np.float64)
CODE_VALUE, SCALE_VALUE = values_of_codes(), 2.0 ** (np.arange(256) - 127.0)
def decode(q):
    return (CODE_VALUE[q[0]].reshape(16, 8, -1, 4) * SCALE_VALUE[q[1]][:, None, :, None] + 0.0).reshape(128, -1).astype(np.float32)
def f(rng, *shape):
    return mx_ref.flush((rng.standard_normal(shape, dtype=np.float32) * np.exp2(rng.integers(-2, 3, shape[:-1] + (1,)))).astype(BF))
def wide(rng, *shape, cols=0):
    v = rng.standard_normal(shape, dtype=np.float32) * np.exp2(rng.integers(-12, 13, shape)).astype(np.float32)
    if cols: v *= np.repeat(np.exp2(rng.integers(-cols, cols + 1, shape[:-2] + (1, shape[-1] // 4))) * (rng.random(shape[:-2] + (1, shape[-1] // 4)) > 0.0625), 4, axis=-1).astype(np.float32)
    return mx_ref.flush(v.astype(BF))
C, K, M, R = 352, 96, 32, 3
STEP = [1, 2, 4]
def order(s, k):
    s, k = s + np.float32(0.0), k + np.float32(0.0)
    best = np.argsort(-s[:, 1:], axis=1, kind="stable")[:, :M - 1] + 1
    head = np.sort(np.concatenate([np.zeros((8, 1), np.int64), best], axis=1), axis=1)
    last = np.concatenate([head[:, 1:] - 1, np.full((8, 1), C - 1)], axis=1)
    key = np.take_along_axis(k, head, axis=1)
    turn = key < np.take_along_axis(k, last, axis=1)
    run = np.argsort(-key, axis=1, kind="stable")
    return np.stack([np.concatenate([np.arange(head[g, n], last[g, n] + 1)[::-1 if turn[g, n] else 1] for n in run[g]]) for g in range(8)])
def strip(v):
    v = v.astype(np.float32)
    v[np.abs(v) < np.float32(2.0 ** -16)] = 0
    return v.astype(BF)
def numbers_of(rng):
    return {"x": strip(f(rng, N, 128, 4 * C)), "u": np.array(f(rng, N, 128, 512)), "v": np.array(f(rng, N, 128, 512))}
def weights(rng, e=slice(0, 0)):
    w = np.array(f(rng, N, 128, 2048)).reshape(N, 8, 16, 4, 8, 16, 4)
    w[:, :, e] = 0
    w[:, :, :, :, :, e] = 0
    c, p = packed(w.reshape(N, 128, 2048), rng)
    return {"wc": c, "ws": p}
def signs(rng):
    return np.stack([rng.permutation(8) % 2 * 2.0 - 1.0 for r in range(N)])
def small(rng):
    return np.where(rng.permutation(N) < N // 2, 2.0 ** -30, 1.0).astype(np.float32)
def setup_inputs(rng):
    return {**numbers_of(rng), **weights(rng)}
def setup_inputs_ties(rng):
    d = numbers_of(rng)
    e = rng.permutation(N)
    x = d["x"].reshape(N, 8, 16, C, 4)
    for r in range(N):
        k = np.zeros(C, int) if r == e[0] else rng.permutation(C) % 3
        a = x[r][:, :8, :3].copy()
        a[:, :, 2] = 0
        x[r][:, :8] = a[:, :, k]
    x[e[1]] = 0
    u = d["u"].reshape(N, 128, 128, 4)
    for g in range(0, 128, 16):
        for h in (g, g + 1):
            a = u[:, g:g + 8, h].copy()
            u[:, :, h] = 0
            u[:, g:g + 8, h] = a
    return {"x": x.reshape(N, 128, 4 * C), "u": u.reshape(N, 128, 512), "v": d["v"], **weights(rng, slice(0, 8))}
def setup_inputs_near(rng):
    d = numbers_of(rng)
    x = d["x"].astype(np.float32).reshape(N, 8, 16, C, 4)
    s = np.zeros((N, 8, C), np.int64)
    s[:, :, 1:] = (1 + np.argsort(rng.random((N, 8, C - 1)), axis=2)) // 2
    k = rng.integers(0, 12, (N, 8, C))
    digit = np.exp2(np.arange(8) - 23.0)
    a = ((s[..., None] >> np.arange(8)) & 1) * digit
    x[:, :, 0] = 0
    x[:, :, 0, :, 0] = signs(rng)[:, :, None]
    x[:, :, 8] = a[..., :4]
    x[:, :, 9] = a[..., 4:]
    x[:, :, 10] = ((k[..., None] >> np.arange(4)) & 1) * digit[:4]
    x[:, :, 11:] = rng.integers(4, 8, (N, 8, 5, C, 4)) * rng.choice([-1.0, 1.0], (N, 8, 5, C, 4)) * 2.0 ** -20
    u = d["u"].reshape(N, 128, 128, 4)
    one = small(rng).astype(BF)
    u[:, :, ::16] = 0
    u[:, :, 1::16] = 0
    for h in range(0, 128, 16):
        u[:, h, h, 0] = one
        u[:, h, h + 1, 0] = one
        u[:, h + 8:h + 10, h] = one[:, None, None]
        u[:, h + 10, h + 1] = one[:, None]
    return {"x": x.reshape(N, 128, 4 * C).astype(BF), "u": u.reshape(N, 128, 512), "v": d["v"], **weights(rng, np.r_[0, 8:16])}
def setup_inputs_runs(rng):
    d = numbers_of(rng)
    x = d["x"].astype(np.float32).reshape(N, 8, 16, C, 4)
    x[:, :, :8] = rng.integers(1, 4, (N, 8, 8, C, 4))
    x[:, :, :2] = 0
    for r in range(N):
        kind = rng.permutation(8)
        for g in range(8):
            i = kind[g] % 4
            lo, hi = ((1, M), (C - M + 1, C), (K + 1, C), (1, C))[i]
            e = lo + rng.permutation(hi - lo)[:M - 1]
            s = rng.integers(-1, 2, C) * 1.0
            s[e] = 1.25
            s[0] = 3
            k = rng.integers(-4, 4, C)
            if i == 0: k = 3 - np.arange(C) * 8 // C
            if i == 1: k = np.arange(C) * 8 // C - 4
            if i == 2:
                k = rng.integers(-4, 2, C) * 1.0
                k[0] = 2
                if kind[g] > 3: k[np.min(e) - 1] = 2.5
            x[r, g, 0, :, 0] = s
            x[r, g, 1, :, 0] = k
    one = small(rng)
    x[:, :, :8] *= one[:, None, None, None, None]
    u = d["u"].reshape(N, 128, 128, 4)
    u[:, :, ::16] = 0
    u[:, :, 1::16] = 0
    for h in range(0, 128, 16):
        u[:, h, h, 0] = one.astype(BF)
        u[:, h + 1, h + 1, 0] = one.astype(BF)
    return {"x": x.reshape(N, 128, 4 * C).astype(BF), "u": u.reshape(N, 128, 512), "v": d["v"], **weights(rng, slice(0, 8))}
def setup_inputs_huge(rng):
    d = numbers_of(rng)
    o = rng.permutation(N)
    x = 0.8 + 0.2 * rng.random((N, 128, C, 4))
    most = np.where(rng.random((128, C, 4)) < 0.03125, 0.9375, 1.0)
    most[:, rng.permutation(C) % 4 == 0] = 1
    x[o == 0] = most
    c = np.stack([rng.permutation(C) % 2 * 2.0 - 1.0 for r in range(N)])
    c[o < N // 2] = 1
    x *= 2.0 ** 30 * c[:, None, :, None]
    u = d["u"].reshape(N, 128, 128, 4)
    for i in range(2):
        a = 1 - 0.125 * rng.random((N, 128, 8, 4))
        a[o == 0] = 1
        a *= 2.0 ** 30 * signs(rng)[:, None, :, None]
        u[:, :, i::16] = a.astype(np.float32).astype(BF)
    return {"x": x.astype(np.float32).reshape(N, 128, 4 * C).astype(BF), "u": u.reshape(N, 128, 512), "v": d["v"], **weights(rng, slice(0, 16))}
def setup_inputs_spread(rng):
    d = setup_inputs(rng)
    d["x"] = strip(wide(rng, N, 128, 4 * C, cols=6))
    return d
def check_inputs(d):
    b = []
    for k in ("x", "u", "v"):
        a = np.abs(d[k].astype(np.float32))
        if not (np.isfinite(a).all() and ((a == 0) | (a >= 2.0 ** -30) & (a <= 2.0 ** 30)).all()): b.append("a value of " + k)
    return b
def reference(x, u, v, wc, ws):
    qu = [mx_ref.quantize(u[r]) for r in range(N)]
    lay = [pk(wc[r], ws[r]) for r in range(N)]
    now = [x[r] for r in range(N)]
    for t in range(R):
        o, border = [], []
        for r in range(N):
            p = mx_ref.matmul(qu[r], mx_ref.quantize(now[r]))
            o.append(order(p[::16], p[1::16]))
            border.append(mx_ref.quantize(gcols(now[r], o[r][:, :K])))
        came = decode(join(*border)).astype(BF)
        for r in range(N):
            e = np.concatenate([cut(came, r ^ STEP[t], 4 * K), gcols(now[r], o[r][:, K:])], axis=1)
            q = mx_ref.quantize(np.ascontiguousarray(e))
            h = [np.maximum(mx_ref.matmul(pick(lay[r], np.arange(128 * b, 128 * b + 128)), q), np.float32(0.0)) * np.float32(0.015625) for b in range(4)]
            now[r] = (e.astype(np.float32) + np.stack(h, axis=2).reshape(128, -1)).astype(BF)
    y, ol = np.zeros((N, 128, C), np.float32), np.zeros((N, 8, C), np.float32)
    oc, osc = np.zeros((N, 128, 4 * C), np.uint8), np.zeros((N, 16, C), np.uint8)
    for r in range(N):
        q = mx_ref.quantize(now[r])
        y[r] = mx_ref.matmul(mx_ref.quantize(v[r]), q)
        ol[r] = o[r]
        oc[r], osc[r] = emit(q)
    return {"y": y, "ol": ol, "oc": oc, "osc": osc}

@@ -1,0 +1,584 @@
+from concourse.mybir import dt, AluOpType as A, AxisListType, ActivationFunctionType as F
+
+C, K, R = 352, 96, 3
+CA = 128
+BIG = 1e29
+MID = 176
+Q, U8, F32, BF, I32, U16 = "float8_e4m3fn_x4", "uint8", "float32", "bfloat16", "int32", "uint16"
+
+
+def _sb(n, d):
+    return ("sbuf", [128, n], d)
+
+
+SCRATCH = {
+    "ps": ("psum", [128, 4096], F32),
+    "X": _sb(4 * C, BF), "Xp": _sb(4 * C, BF), "E": _sb(4 * C, BF), "Dp": _sb(4 * C, BF),
+    "ut": _sb(512, BF), "vt": _sb(512, BF), "zt": _sb(C, BF), "et": _sb(2048, BF), "pj": _sb(128, F32), "id": _sb(128, BF),
+    "uq": _sb(128, Q), "us": _sb(128, U8), "u2q": _sb(256, Q), "u2s": _sb(256, U8),
+    "vq": _sb(128, Q), "vs": _sb(128, U8), "wq": _sb(512, Q), "wp": _sb(512, U8),
+    "eq": _sb(512, Q), "es": _sb(512, U8), "xq": _sb(C, Q), "xs": _sb(C, U8), "hq": _sb(384, Q), "hs": _sb(384, U8),
+    "rq": _sb(C, Q), "rs": _sb(C, U8), "rl": _sb(6, U16),
+    "Rl": _sb(1536, F32), "yb": _sb(C, F32), "ob": _sb(C, F32),
+    "srow": _sb(448, F32), "krow": _sb(360, F32), "ksh": _sb(360, F32),
+    "M": _sb(384, F32), "Mm": _sb(96, F32), "p1": _sb(96, F32),
+    "c1": _sb(352, BF), "n1": _sb(352, BF), "sa": _sb(384, BF), "sj": _sb(384, BF), "na": _sb(8, F32),
+    "o1": _sb(8, U16), "f1": _sb(112, BF), "q1": _sb(112, BF), "v1": _sb(96, F32), "t1": _sb(8, F32),
+    "nb": _sb(8, F32), "oc4": _sb(8, U16), "cand": _sb(128, F32), "cm": _sb(128, F32), "p2": _sb(128, F32),
+    "c2": _sb(640, BF), "n2": _sb(640, BF), "nc": _sb(8, F32), "o2": _sb(8, U16), "v2": _sb(128, F32),
+    "gt": _sb(C, BF), "sg": _sb(C, BF), "ge": _sb(C, BF), "pg": _sb(C + 8, BF), "pp": _sb(C, BF),
+    "le": _sb(C, BF), "lc": _sb(C, BF),
+    "nd": _sb(8, F32), "o3": _sb(2, U16), "kb": _sb(40, F32), "kl": _sb(32, F32), "km": _sb(40, F32),
+    "eb": _sb(40, F32), "p3": _sb(32, F32), "ln": _sb(32, F32), "lm": _sb(32, F32), "tn": _sb(32, F32),
+    "t2": _sb(32, F32), "ff": _sb(32, BF), "dd": _sb(32, BF), "c3": _sb(96, F32), "wt": _sb(96, F32),
+    "m3": _sb(96, F32), "n3": _sb(96, F32), "o4": _sb(2, U16), "dv": _sb(C, BF), "row": _sb(384, BF),
+    "w1": _sb(224, BF), "w2": _sb(544, BF), "ob1": _sb(16, U16), "ob2": _sb(16, U16),
+    "mw": _sb(R * C, BF), "dw": _sb(R * C, BF), "z32": _sb(32, BF),
+    "ci": _sb(8, I32), "cf": _sb(16, F32), "pi": _sb(16, I32), "pl": _sb(16, U16), "j16": _sb(128, F32),
+    "hot": _sb(128, F32), "s16": _sb(128, F32), "s4": _sb(C, F32), "s88": _sb(352, BF), "s128": _sb(640, BF),
+    "s48": _sb(96, F32), "tf": _sb(96, BF), "tb": _sb(96, F32), "tc": _sb(128, F32), "iw": _sb(360, F32),
+    "tri": _sb(96, F32), "wl": _sb(10, U16), "wf": _sb(8, F32), "rb": _sb(4, F32),
+}
+for _t in range(R):
+    SCRATCH["lq%d" % _t] = _sb(C, Q)
+    SCRATCH["ls%d" % _t] = _sb(C, U8)
+    SCRATCH["ll%d" % _t] = _sb(6, U16)
+SEMAPHORES = (["cv", "ca", "ct", "cg", "sent", "hq", "hs", "hl"]
+              + [n + str(t) for n in ("aq", "as", "al", "sq", "ss", "sl") for t in range(R)] + ["d%d" % i for i in range(24)])
+
+
+def bits(engines):
+    return sum(1 << e for e in engines)
+
+
+def helpers(topo, src, dst):
+    h = [c for c in topo.cores_of(src) if c != src and topo.may_write(c, dst)]
+    return sorted(h, key=lambda c: topo.die(c) != topo.die(src))[:2]
+
+
+def far_engines(topo, cores, r):
+    for t in range(R):
+        if topo.may_write(cores[r], cores[r ^ (1 << t)]):
+            return topo.engines(cores[r], cores[r ^ (1 << t)])
+    return topo.engines(cores[r], helpers(topo, cores[r], cores[r ^ 1])[0])
+
+
+def counts(topo, cores, r, t):
+    p = r ^ (1 << t)
+    if topo.may_write(cores[p], cores[r]):
+        n = len(far_engines(topo, cores, p))
+        return n, n, n
+    h = helpers(topo, cores[p], cores[r])
+    n = len(topo.engines(h[1], cores[r]))
+    return len(topo.engines(h[0], cores[r])), n, n
+
+
+def hand_on(g, core, T, topo):
+    cores = T.cores
+    for t in range(R):
+        for r in range(len(cores)):
+            src, dst = cores[r], cores[r ^ (1 << t)]
+            if topo.may_write(src, dst):
+                continue
+            h = helpers(topo, src, dst)
+            if core not in h:
+                continue
+            n = len(far_engines(topo, cores, r))
+            rid, pid = topo.addr(dst, core)
+            e = topo.engines(core, dst)
+            if core == h[0]:
+                g.wait_ge(T.sem.hq, n)
+                g.remote_dma(T["lq%d" % t][:].bitcast(dt.uint8), T.rq[:].bitcast(dt.uint8), T.sem["aq%d" % t], T.sem.sent, pid, rid, bits(e))
+                g.wait_ge(T.sem.sent, len(e))
+            else:
+                g.wait_ge(T.sem.hs, n)
+                g.remote_dma(T["ls%d" % t][:], T.rs[:], T.sem["as%d" % t], T.sem.sent, pid, rid, bits(e))
+                g.wait_ge(T.sem.hl, n)
+                g.remote_dma(T["ll%d" % t][:], T.rl[:], T.sem["al%d" % t], T.sem.sent, pid, rid, bits(e))
+                g.wait_ge(T.sem.sent, 2 * len(e))
+
+
+def rank_program(g, core, T, topo):
+    rank = T.rank_of(core)
+    if rank is None:
+        hand_on(g, core, T, topo)
+        return
+    cores = T.cores
+    queue = {"v": g.vector, "a": g.scalar, "t": g.tensor, "g": g, "s": g.sync}
+    csem = {"v": "cv", "a": "ca", "t": "ct", "g": "cg"}
+    done = {k: 0 for k in csem}
+    clock = {k: {} for k in queue}
+    past = {}
+    dmas = []
+    sent = []
+    seqno = [0]
+
+    def V(name, lo=0, hi=None, step=1):
+        t = T[name]
+        if hi is None:
+            hi = t.shape[1]
+        m = 0
+        for c in range(lo, hi, step):
+            m |= 1 << c
+        return (t[:, lo:hi:step] if step > 1 else t[:, lo:hi], name, m)
+
+    def col(name, c):
+        return V(name, c, c + 1)
+
+    def P(bank, lo, hi):
+        return (T.ps[:, 512 * bank + lo:512 * bank + hi], "ps", 1 << bank)
+
+    def IND(win, off):
+        return (win[0].indirect(off[0]), win[1], win[2], off)
+
+    def order(e, outs, ins):
+        acc = [(v[1], v[2], True) for v in outs] + [(v[1], v[2], False) for v in ins]
+        acc += [(v[3][1], v[3][2], False) for v in list(outs) + list(ins) if len(v) > 3]
+        need = []
+        for name, m, w in acc:
+            for (m2, w2, e2, ev, ck, seq) in past.get(name, []):
+                if m & m2 and (w or w2 or (name == "ps" and e2 != e)):
+                    need.append((seq, ev, ck))
+        need.sort(key=lambda x: -x[0])
+        for seq, ev, ck in need:
+            if clock[e].get(ev[0], 0) >= ev[1]:
+                continue
+            queue[e].wait_ge(T.sem[ev[0]], ev[1])
+            clock[e][ev[0]] = ev[1]
+            for k2, n2 in ck.items():
+                if clock[e].get(k2, 0) < n2:
+                    clock[e][k2] = n2
+        return acc
+
+    def note(e, acc, ev, ck):
+        seqno[0] += 1
+        for name, m, w in acc:
+            old = past.get(name, [])
+            if w:
+                old = [o for o in old if o[0] & ~m]
+            past[name] = old + [(m, w, e, ev, ck, seqno[0])]
+
+    def op(e, call, outs, ins):
+        acc = order(e, outs, ins)
+        done[e] += 1
+        call().then_inc(T.sem[csem[e]], 1)
+        note(e, acc, (csem[e], done[e]), dict(clock[e]))
+
+    def dma(e, out, in_, outs, ins):
+        acc = order(e, outs, ins)
+        s = "d%d" % len(dmas)
+        dmas.append(s)
+        queue[e].dma_start(out, in_).then_inc(T.sem[s], 16)
+        note("dma", acc, (s, 16), dict(clock[e]))
+
+    def sc(x):
+        return x[0] if isinstance(x, tuple) else x
+
+    def aps(*xs):
+        return [x for x in xs if isinstance(x, tuple)]
+
+    def ms(o, c):
+        op("v", lambda: g.vector.memset(o[0], c), [o], [])
+
+    def cp(o, i):
+        op("v", lambda: g.vector.tensor_copy(o[0], i[0]), [o], [i])
+
+    def tt(o, a, b, f):
+        op("v", lambda: g.vector.tensor_tensor(o[0], a[0], b[0], f), [o], [a, b])
+
+    def ts(o, a, s1, f1, s2=None, f2=None):
+        if f2 is None:
+            op("v", lambda: g.vector.tensor_scalar(o[0], a[0], sc(s1), None, f1), [o], aps(a, s1))
+        else:
+            op("v", lambda: g.vector.tensor_scalar(o[0], a[0], sc(s1), sc(s2), f1, f2), [o], aps(a, s1, s2))
+
+    def scan(o, a, b, init, f0, f1):
+        op("v", lambda: g.vector.tensor_tensor_scan(o[0], a[0], b[0], sc(init), f0, f1), [o], aps(a, b, init))
+
+    def red(o, a, f):
+        op("v", lambda: g.vector.tensor_reduce(o[0], a[0], AxisListType.X, f), [o], [a])
+
+    def tr(o, a):
+        op("v", lambda: g.vector.transpose(o[0], a[0]), [o], [a])
+
+    def quant(q, s, a):
+        op("v", lambda: g.vector.quantize_mx(q[0], s[0], a[0]), [q, s], [a])
+
+    def act(o, a, f, bias=None, scale=None, acc=None):
+        kw = {}
+        if bias is not None:
+            kw["bias"] = sc(bias)
+        if scale is not None:
+            kw["scale"] = sc(scale)
+        if acc is not None:
+            kw["accum_out"] = acc[0]
+        op("a", lambda: g.scalar.activation(o[0], a[0], f, **kw), aps(o, acc), aps(a, bias, scale))
+
+    def mm(o, wq, ws, xq, xs):
+        op("t", lambda: g.tensor.matmul_mx(o[0], wq[0], ws[0], xq[0], xs[0], True, True), [o], [wq, ws, xq, xs])
+
+    def iota(o, pattern, base, cm, small=True):
+        if small:
+            op("g", lambda: g.iota(o[0], pattern, base, cm, allow_small_or_imprecise_dtypes=True), [o], [])
+        else:
+            op("g", lambda: g.iota(o[0], pattern, base, cm), [o], [])
+
+    def direct(t):
+        return topo.may_write(core, cores[rank ^ (1 << t)])
+
+    def ship(t, k):
+        partner = cores[rank ^ (1 << t)]
+        src = (V("xq"), V("xs"), V("ob1", 0, 6))[k]
+        c = "qsl"[k]
+        if direct(t):
+            land, dst, sem = T["l" + c + str(t)][:], partner, "a" + c + str(t)
+        else:
+            land, dst, sem = T["r" + c][:], helpers(topo, core, partner)[min(k, 1)], "h" + c
+        eng = far_engines(topo, cores, rank)
+        acc = order("g", [], [src])
+        rid, pid = topo.addr(dst, core)
+        g.remote_dma(land.bitcast(dt.uint8) if k == 0 else land, src[0].bitcast(dt.uint8) if k == 0 else src[0],
+                     T.sem[sem], T.sem["s" + c + str(t)], pid, rid, bits(eng))
+        sent.append(("s" + c + str(t), len(eng)))
+        note("far", acc, sent[-1], dict(clock["g"]))
+        note("far", [V("l" + c + str(t))[1:] + (True,)], ("a" + c + str(t), counts(topo, cores, rank, t)[k]), {})
+
+    dma("s", T.ut[:], T.u[:], [V("ut")], [])
+    dma("a", T.X[:, 4 * CA:4 * C], T.x[:, 4 * CA:4 * C], [V("X", 4 * CA)], [])
+    dma("s", T.X[:, 0:4 * CA], T.x[:, 0:4 * CA], [V("X", 0, 4 * CA)], [])
+    iota(V("pi"), [[1, 2], [16, 8]], 0, 0, False)
+    iota(V("j16"), [[0, 8], [1, 16]], 0, 0)
+    iota(col("ci", 0), [[0, 1]], 0, 1, False)
+    iota(V("pj"), [[-1, 128]], 0, 1)
+    iota(V("s88"), [[0, 4], [256, 88]], 0, 0)
+    iota(V("iw"), [[1, 360]], -MID, 0)
+    iota(V("s48"), [[0, 2], [512, 48]], 0, 0)
+    iota(V("wf", 0, 6), [[0, 3], [16, 2]], 0, 0)
+
+    def fill(o, c, n):
+        act(o, V("j16", 0, n), F.Identity, bias=c, scale=0.0)
+
+    ms(V("et"), 0.0)
+    ts(col("ci", 1), col("ci", 0), 15, A.bitwise_and)
+    ts(col("ci", 2), col("ci", 0), 4, A.logical_shift_right)
+    cp(V("pl"), V("pi"))
+    ms(V("s128"), 1.0)
+    cp(col("cf", 0), col("ci", 1))
+    tt(col("ci", 3), col("ci", 0), col("ci", 2), A.add)
+    ms(V("zt"), 0.0)
+    ts(V("hot"), V("j16"), col("cf", 0), A.is_equal)
+    ts(col("ci", 4), col("ci", 3), 1, A.bitwise_and)
+    ms(V("s128", 0, 640, 128), 0.0)
+    ts(V("s16"), V("j16"), 0.5, A.is_gt)
+    cp(col("cf", 1), col("ci", 4))
+    ts(col("cf", 2), col("cf", 0), 5.0, A.min, 16.0, A.mult)
+    ts(V("id"), V("pj"), 0.0, A.is_equal)
+    for b in (1, 2, 3):
+        fill(V("s4", b, C, 4), BIG, 88)
+    fill(V("s4", 0, C, 4), -BIG, 88)
+    for o, x, n in ((V("M", C), -BIG, 32), (col("srow", 0), BIG, 1), (V("f1", 96), 0.0, 16), (V("tf", 0, 57), 0.0, 57),
+                    (V("tf", 57), 1.0, 39), (V("tb", 0, 57), BIG, 57), (V("tb", 57), -BIG, 39), (V("tc", 0, 32), -BIG, 32),
+                    (V("tc", 32), BIG, 96), (V("krow", C), 0.0, 8), (col("ksh", 0), 0.0, 1), (V("ksh", C + 1), 0.0, 7),
+                    (V("pg", C), 32.0, 8), (col("eb", 0), float(-MID), 1), (V("z32"), 0.0, 32), (V("row", 0, 16), 0.0, 16),
+                    (V("row", 16 + C), 0.0, 16), (V("tri", 16, 32), 1.0, 16), (V("tri", 64, 80), 1.0, 16)):
+        fill(o, x, n)
+    act(V("wt", 0, 16), V("j16", 0, 16), F.Sign, bias=col("cf", 0), scale=-1.0)
+    act(V("Mm", 88), V("hot", 8, 16), F.Identity, scale=-BIG)
+    for c, x in enumerate((-0.5, -16.5, -1.5)):
+        act(col("rb", c), col("cf", 0), F.Identity, bias=x, scale=-1.0)
+    for c in (32, 80):
+        act(V("tri", c, c + 16), V("wt", 0, 16), F.Relu)
+    quant(V("uq"), V("us"), V("ut"))
+
+    def pick_u(k):
+        o, l = V("u2q", 128 * k, 128 * k + 128), V("pl", 8 * k, 8 * k + 8)
+        op("v", lambda: g.vector.tensor_copy(o[0].bitcast(dt.uint32), T.uq[:].bitcast(dt.uint32).indirect(l[0])), [o], [V("uq"), l])
+        act(V("u2s", 128 * k, 128 * k + 128), IND(V("us"), l), F.Copy)
+
+    def late_constants():
+        act(col("rb", 3), col("cf", 0), F.Identity, bias=17.5)
+        act(col("cf", 3), col("cf", 0), F.Identity, scale=16.0)
+        for c in (0, 48):
+            act(V("tri", c, c + 16), V("tri", c + 32, c + 48), F.Identity, bias=1.0, scale=-1.0)
+
+    XB = (V("xq", CA), V("xs", CA))
+    XA = (V("xq", 0, CA), V("xs", 0, CA))
+    US = (V("u2q", 0, 128), V("u2s", 0, 128))
+    UK = (V("u2q", 128), V("u2s", 128))
+    nB = C - CA
+
+    def quant_xb():
+        quant(XB[0], XB[1], V("X", 4 * CA))
+
+    def quant_xa():
+        quant(XA[0], XA[1], V("X", 0, 4 * CA))
+
+    def mm_sb():
+        mm(P(4, 0, nB), US[0], US[1], XB[0], XB[1])
+        mm(P(5, 0, nB), UK[0], UK[1], XB[0], XB[1])
+
+    def mm_sa():
+        mm(P(6, 0, CA), US[0], US[1], XA[0], XA[1])
+        mm(P(7, 0, CA), US[0], US[1], XA[0], XA[1])
+        mm(P(0, 0, CA), UK[0], UK[1], XA[0], XA[1])
+
+    def copy_sb():
+        act(V("srow", CA, C), P(4, 0, nB), F.Copy)
+
+    def copy_kb():
+        act(V("krow", CA, C), P(5, 0, nB), F.Copy)
+        act(V("ksh", CA + 1, C + 1), P(5, 0, nB), F.Copy)
+
+    def scan_mb():
+        scan(V("M", CA, C), V("s4", CA, C), V("srow", CA, C), -BIG, A.min, A.max)
+
+    def scan_ma():
+        scan(V("M", 1, CA), V("s4", 1, CA), P(6, 1, CA), BIG, A.min, A.max)
+        act(V("srow", 1, CA), P(7, 1, CA), F.Copy)
+
+    def plane(b):
+        act(V("Xp", C * b, C * b + C), V("X", b, 4 * C, 4), F.Copy)
+
+    def unpack(t):
+        for b in range(4):
+            mm(P(4 + b, 0, C), V("eq", 128 * b, 128 * b + 128), V("es", 128 * b, 128 * b + 128), V("lq%d" % t), V("ls%d" % t))
+        for b in range(4):
+            act(V("Dp", C * b, C * b + C), P(4 + b, 0, C), F.Copy)
+
+    def sort(t):
+        Mv = V("M", 3, C, 4)
+        tt(V("Mm", 0, 88), Mv, V("hot", 0, 88), A.mult)
+        scan(V("p1"), V("s16", 0, 96), V("Mm"), 0.0, A.mult, A.add)
+        for m in range(4):
+            ts(V("c1", 88 * m, 88 * m + 88), Mv, col("p1", 16 * m + 15), A.is_lt)
+        for m in (4, 5):
+            act(V("sa", 128 * (m - 4), 128 * (m - 4) + 88), Mv, F.Sign, bias=col("p1", 16 * m + 15), scale=-1.0)
+        for m in (4, 5):
+            act(V("sj", 128 * (m - 4), 128 * (m - 4) + 88), V("sa", 128 * (m - 4), 128 * (m - 4) + 88), F.Relu, acc=col("na", m))
+        act(V("krow", 0, CA), P(0, 0, CA), F.Copy)
+        act(V("ksh", 1, CA + 1), P(0, 0, CA), F.Copy)
+        if t == 0:
+            late_constants()
+        else:
+            plane(0)
+        scan(V("n1"), V("s88"), V("c1"), 0.0, A.min, A.add)
+        cp(V("o1", 4, 6), V("na", 4, 6))
+        cp(V("o1", 0, 4), V("n1", 87, 352, 88))
+        cp(V("f1", 0, 96), IND(V("tf"), V("o1", 0, 6)))
+        scan(V("q1", 0, 110), V("f1", 0, 110), V("f1", 0, 110), 0.0, A.add, A.max)
+        for m in range(2):
+            act(V("sj", 128 * m, 128 * m + 110), V("q1", 0, 110), F.Sign, bias=col("rb", m), acc=col("nb", m))
+        plane(1)
+        tt(V("v1"), IND(V("tb"), V("o1", 0, 6)), V("M", 3, 384, 4), A.min)
+        scan(V("srow", C), V("v1"), V("v1"), -BIG, A.max, A.max)
+        for b in range(4):
+            ts(V("oc4", 2 * b, 2 * b + 2), V("nb", 0, 2), -2.0, A.mult, float(220 + b), A.add)
+        act(V("cand"), IND(V("srow"), V("oc4")), F.Copy)
+        tt(V("cm"), IND(V("srow"), V("oc4")), V("hot"), A.mult)
+        if t == 0:
+            ts(V("wl", 0, 6), V("wf", 0, 6), col("cf", 0), A.add)
+        scan(V("p2"), V("s16"), V("cm"), 0.0, A.mult, A.add)
+        if t == 0:
+            ts(col("wl", 6), col("cf", 1), 112.0, A.mult, col("cf", 2), A.add)
+        for m in range(5):
+            ts(V("c2", 128 * m, 128 * m + 128), V("cand"), col("p2", 16 * m + 15), A.is_gt)
+        for m in (5, 6, 7):
+            act(V("sa", 128 * (m - 5), 128 * (m - 4)), V("cand"), F.Sign, bias=col("p2", 16 * m + 15), scale=-1.0)
+        for m in (5, 6, 7):
+            act(V("sj", 128 * (m - 5), 128 * (m - 4)), V("sa", 128 * (m - 5), 128 * (m - 4)), F.Relu, scale=-1.0, acc=col("nc", m))
+        plane(2)
+        if t == 0:
+            plane(0)
+            ts(col("wl", 8), col("cf", 1), 272.0, A.mult, col("cf", 3), A.add)
+        scan(V("n2"), V("s128"), V("c2"), 0.0, A.mult, A.add)
+        cp(V("o2", 5, 8), V("nc", 5, 8))
+        cp(V("o2", 0, 5), V("n2", 127, 640, 128))
+        tt(V("v2"), IND(V("tc"), V("o2")), V("cand"), A.max)
+        red(col("t1", 0), V("v2"), A.min)
+        S = V("srow", 0, C)
+        ts(V("gt"), S, col("t1", 0), A.is_gt, -1.0, A.mult)
+        act(V("sg"), S, F.Sign, bias=col("t1", 0), scale=-1.0)
+        act(V("ge", MID), V("sg", MID), F.Sign, bias=1.0, scale=-1.0)
+        back = [(T[n][:, C - 1:0:-1],) + V(n, 1, C)[1:] for n in ("pg", "gt")]
+        scan(back[0], back[1], back[1], 32.0, A.add, A.max)
+        ts(V("ge", 0, MID), V("sg", 0, MID), 0.5, A.is_lt)
+        scan(V("pp"), V("ge"), V("pg", 1, C + 1), 0.0, A.add, A.min)
+        act(V("sg"), V("pp"), F.Sign, bias=col("rb", 2), acc=col("nd", 0))
+        act(col("kb", 0), col("krow", 0), F.Copy)
+        act(col("km", 0), col("krow", 0), F.Copy, scale=col("hot", 0))
+        ts(V("le"), V("pp"), col("rb", 3), A.is_le)
+        scan(V("lc"), V("le"), V("zt"), float(-MID), A.add, A.add)
+        ts(col("o3", 0), col("nd", 0), -0.5, A.mult, 176.0, A.add)
+        ts(col("o3", 1), col("lc", C - 1), float(MID), A.add)
+        tt(V("km", 1, 33), IND(V("krow"), V("o3")), V("hot", 1, 33), A.mult)
+        act(V("eb", 1, 33), IND(V("iw"), V("o3")), F.Copy)
+        act(V("kb", 1, 33), IND(V("krow"), V("o3")), F.Copy)
+        act(V("kl"), IND(V("ksh"), V("o3")), F.Copy)
+        scan(V("p3"), V("s16", 0, 32), V("km", 0, 32), 0.0, A.mult, A.add)
+        tt(V("ln"), V("eb", 1, 33), V("eb", 0, 32), A.subtract)
+        act(V("lm"), V("ln"), F.Identity, bias=-1.0)
+        ts(V("c3", 0, 32), V("kb", 0, 32), col("p3", 15), A.is_gt)
+        tt(V("wt"), IND(V("ln"), V("wl", 0, 6)), V("tri"), A.mult)
+        ts(V("c3", 32, 48), V("kb", 0, 16), col("p3", 15), A.is_ge)
+        ts(V("c3", 48, 64), V("kb", 16, 32), col("p3", 31), A.is_gt)
+        ts(V("c3", 64, 96), V("kb", 0, 32), col("p3", 31), A.is_ge)
+        tt(V("tn"), V("kb", 0, 32), V("kl"), A.is_lt)
+        tt(V("m3"), V("c3"), V("wt"), A.mult)
+        act(V("dd"), V("tn"), F.Identity, bias=1.0, scale=-2.0)
+        plane(3)
+        if t == 0:
+            for b in range(4):
+                act(V("et", 512 * b + b, 512 * b + 512, 4), V("id"), F.Copy)
+        if direct(t):
+            if t == 0:
+                quant(V("eq"), V("es"), V("et"))
+            unpack(t)
+        tt(V("t2"), V("lm"), V("tn"), A.mult)
+        scan(V("n3"), V("s48"), V("m3"), 0.0, A.min, A.add)
+        tt(V("ff"), V("t2"), V("eb", 0, 32), A.add)
+        cp(V("o4"), V("n3", 47, 96, 48))
+        mw, dw = V("mw", C * t, C * t + C), V("dw", C * t, C * t + C)
+        cp(IND(mw, V("o4")), V("z32"))
+        cp(IND(dw, V("o4")), V("dd"))
+        scan(V("dv"), mw, dw, 0.0, A.mult, A.add)
+        cp(IND(V("dv"), V("o4")), V("ff"))
+        scan(V("row", 16, 16 + C), mw, V("dv"), 0.0, A.mult, A.add)
+        tr(V("w1", 0, 96), V("row", 16, 112))
+        tr(V("w1", 96), V("row", 0, 128))
+        ts(V("ob1"), IND(V("w1"), col("wl", 6)), float(MID), A.add)
+
+    def pick(e, o, win, b, off):
+        src = IND(V(win, C * b, C * b + C), off)
+        if e == "v":
+            cp(o, src)
+        else:
+            act(o, src, F.Copy)
+
+    LO, NEW, BANK = (0, K, K + 128), (K, 128, 128), (0, 0, 4)
+
+    def layer(k):
+        q, s = V("hq", 128 * k, 128 * k + 128), V("hs", 128 * k, 128 * k + 128)
+        quant(q, s, V("E", 4 * LO[k], 4 * LO[k] + 512))
+        for b in range(4):
+            mm(P(BANK[k] + b, 0, 128), V("wq", 128 * b, 128 * b + 128), V("wp", 128 * b, 128 * b + 128), q, s)
+
+    def rl(k, b):
+        return V("Rl", 512 * k + 128 * b, 512 * k + 128 * b + NEW[k])
+
+    def relu(k):
+        for b in range(4):
+            act(rl(k, b), P(BANK[k] + b, 0, NEW[k]), F.Relu, scale=0.015625)
+
+    def add(k, b):
+        lo, hi = 4 * LO[k] + b, 4 * (LO[k] + NEW[k])
+        tt(V("X", lo, hi, 4), V("E", lo, hi, 4), rl(k, b), A.add)
+
+    def swap(t):
+        last = t == R - 1
+        ship(t, 2)
+        if not last:
+            iota(V("mw", C * t + C, C * t + 2 * C), [[0, C]], 1, 0)
+            iota(V("dw", C * t + C, C * t + 2 * C), [[0, C]], 0, 0)
+        tr(V("w2", 0, 256), V("row", 112, 368))
+        tr(V("w2", 256), V("row", 96, 384))
+        ts(V("ob2"), IND(V("w2"), col("wl", 8)), float(MID), A.add)
+        for k in (1, 2):
+            for b in range(4):
+                pick("av"[b // 2], V("E", 4 * LO[k] + b, 4 * LO[k] + 512, 4), "Xp", b, V("ob2", 8 * k - 8, 8 * k))
+            layer(k)
+        relu(1)
+        relu(2)
+
+        def border():
+            for b in range(4):
+                pick("a" if direct(t) or b < 2 else "v", V("E", b, 4 * K, 4), "Dp", b, V("ll%d" % t))
+
+        def scores_b():
+            quant_xb()
+            if last:
+                mm(P(4, 0, nB), V("vq"), V("vs"), XB[0], XB[1])
+                dma("s", T.oc[:, 4 * CA:4 * C], T.xq[:, CA:C].bitcast(dt.uint8), [], [XB[0]])
+                act(V("yb", CA), P(4, 0, nB), F.Copy)
+                dma("s", T.y[:, CA:C], T.yb[:, CA:C], [], [V("yb", CA)])
+            else:
+                mm_sb()
+                copy_sb()
+                copy_kb()
+
+        if direct(t):
+            border()
+            for b in range(4):
+                add(1, b)
+            for b in range(3):
+                add(2, b)
+            layer(0)
+            relu(0)
+            add(2, 3)
+            scores_b()
+        else:
+            add(1, 0)
+            if t == 0:
+                quant(V("eq"), V("es"), V("et"))
+            unpack(t)
+            for k, b in ((1, 1), (1, 2), (1, 3), (2, 0), (2, 1), (2, 2), (2, 3)):
+                add(k, b)
+            scores_b()
+            if not last:
+                scan_mb()
+            if t == 0:
+                quant(V("vq"), V("vs"), V("vt"))
+            border()
+            layer(0)
+            relu(0)
+        if direct(t) and t == 0:
+            quant(V("vq"), V("vs"), V("vt"))
+        if last:
+            act(V("ob"), V("row", 16, 16 + C), F.Identity, bias=float(MID))
+            dma("s", T.ol[:], T.ob[0:128:16, :], [], [V("ob")])
+        for b in range(4):
+            add(0, b)
+        quant_xa()
+        if last:
+            mm(P(6, 0, CA), V("vq"), V("vs"), XA[0], XA[1])
+            dma("s", T.oc[:, 0:4 * CA], T.xq[:, 0:CA].bitcast(dt.uint8), [], [XA[0]])
+            for k in range(4):
+                dma("as"[k // 2], T.osc[4 * k:4 * k + 4, :], T.xs[32 * k:32 * k + 4, :], [], [V("xs")])
+            cp(V("yb", 0, CA), P(6, 0, CA))
+            dma("a", T.y[:, 0:CA], T.yb[:, 0:CA], [], [V("yb", 0, CA)])
+        else:
+            mm_sa()
+            ship(t + 1, 0)
+            ship(t + 1, 1)
+            if direct(t):
+                scan_mb()
+            scan_ma()
+
+    pick_u(0)
+    quant_xb()
+    mm(P(4, 0, nB), US[0], US[1], XB[0], XB[1])
+    quant_xa()
+    mm(P(6, 0, CA), US[0], US[1], XA[0], XA[1])
+    mm(P(7, 0, CA), US[0], US[1], XA[0], XA[1])
+    ship(0, 0)
+    ship(0, 1)
+    pick_u(1)
+    mm(P(5, 0, nB), UK[0], UK[1], XB[0], XB[1])
+    mm(P(0, 0, CA), UK[0], UK[1], XA[0], XA[1])
+    dma("s", T.wq[:].bitcast(dt.uint8), T.wc[:], [V("wq")], [])
+    dma("s", T.wp[:], T.ws[:], [V("wp")], [])
+    dma("s", T.vt[:], T.v[:], [V("vt")], [])
+    iota(V("mw", 0, C), [[0, C]], 1, 0)
+    iota(V("dw", 0, C), [[0, C]], 0, 0)
+    copy_sb()
+    scan_mb()
+    scan_ma()
+    copy_kb()
+    for t in range(R):
+        sort(t)
+        swap(t)
+    for s, n in sent:
+        g.wait_ge(T.sem[s], n)
+    for e in csem:
+        g.wait_ge(T.sem[csem[e]], done[e])
+    for s in dmas:
+        g.wait_ge(T.sem[s], 16)

@@ -21,7 +21,8 @@ SCRATCH = {
     "rq": _sb(C, Q), "rs": _sb(C, U8), "rl": _sb(6, U16),
     "Rl": _sb(1536, F32), "yb": _sb(C, F32), "ob": _sb(C, F32),
     "srow": _sb(448, F32), "krow": _sb(360, F32), "ksh": _sb(360, F32),
-    "M": _sb(384, F32), "Mm": _sb(96, F32), "p1": _sb(96, F32),
+    "M": _sb(384, F32), "Mm": _sb(CA, F32), "p1": _sb(CA, F32), "h4": _sb(CA, F32), "s64": _sb(CA, F32),
+    "Mn": _sb(64, F32), "pb": _sb(64, F32),
     "c1": _sb(352, BF), "n1": _sb(352, BF), "sa": _sb(384, BF), "sj": _sb(384, BF), "na": _sb(8, F32),
     "o1": _sb(8, U16), "f1": _sb(112, BF), "q1": _sb(112, BF), "v1": _sb(96, F32), "t1": _sb(8, F32),
     "nb": _sb(8, F32), "oc4": _sb(8, U16), "cand": _sb(128, F32), "cm": _sb(128, F32), "p2": _sb(128, F32),
@@ -56,17 +57,10 @@ def helpers(topo, src, dst):
     return sorted(h, key=lambda c: topo.die(c) != topo.die(src))[:2]
 
 
-def far_engines(topo, cores, r):
-    for t in range(R):
-        if topo.may_write(cores[r], cores[r ^ (1 << t)]):
-            return topo.engines(cores[r], cores[r ^ (1 << t)])
-    return topo.engines(cores[r], helpers(topo, cores[r], cores[r ^ 1])[0])
-
-
 def counts(topo, cores, r, t):
     p = r ^ (1 << t)
     if topo.may_write(cores[p], cores[r]):
-        n = len(far_engines(topo, cores, p))
+        n = len(topo.engines(cores[p], cores[r]))
         return n, n, n
     h = helpers(topo, cores[p], cores[r])
     n = len(topo.engines(h[1], cores[r]))
@@ -83,7 +77,7 @@ def hand_on(g, core, T, topo):
             h = helpers(topo, src, dst)
             if core not in h:
                 continue
-            n = len(far_engines(topo, cores, r))
+            n = len(topo.engines(src, core))
             rid, pid = topo.addr(dst, core)
             e = topo.engines(core, dst)
             if core == h[0]:
@@ -234,7 +228,7 @@ def rank_program(g, core, T, topo):
             land, dst, sem = T["l" + c + str(t)][:], partner, "a" + c + str(t)
         else:
             land, dst, sem = T["r" + c][:], helpers(topo, core, partner)[min(k, 1)], "h" + c
-        eng = far_engines(topo, cores, rank)
+        eng = topo.engines(core, dst)
         acc = order("g", [], [src])
         rid, pid = topo.addr(dst, core)
         g.remote_dma(land.bitcast(dt.uint8) if k == 0 else land, src[0].bitcast(dt.uint8) if k == 0 else src[0],
@@ -249,10 +243,8 @@ def rank_program(g, core, T, topo):
     iota(V("pi"), [[1, 2], [16, 8]], 0, 0, False)
     iota(V("j16"), [[0, 8], [1, 16]], 0, 0)
     iota(col("ci", 0), [[0, 1]], 0, 1, False)
-    iota(V("pj"), [[-1, 128]], 0, 1)
     iota(V("s88"), [[0, 4], [256, 88]], 0, 0)
-    iota(V("iw"), [[1, 360]], -MID, 0)
-    iota(V("s48"), [[0, 2], [512, 48]], 0, 0)
+    iota(V("pj"), [[-1, 128]], 0, 1)
     iota(V("wf", 0, 6), [[0, 3], [16, 2]], 0, 0)
 
     def fill(o, c, n):
@@ -272,18 +264,22 @@ def rank_program(g, core, T, topo):
     ts(V("s16"), V("j16"), 0.5, A.is_gt)
     cp(col("cf", 1), col("ci", 4))
     ts(col("cf", 2), col("cf", 0), 5.0, A.min, 16.0, A.mult)
+    for b in range(4):
+        ts(V("h4", b, CA, 4), V("hot", 0, 32), 2 * BIG, A.mult, -BIG, A.add)
     ts(V("id"), V("pj"), 0.0, A.is_equal)
     for b in (1, 2, 3):
         fill(V("s4", b, C, 4), BIG, 88)
     fill(V("s4", 0, C, 4), -BIG, 88)
-    for o, x, n in ((V("M", C), -BIG, 32), (col("srow", 0), BIG, 1), (V("f1", 96), 0.0, 16), (V("tf", 0, 57), 0.0, 57),
-                    (V("tf", 57), 1.0, 39), (V("tb", 0, 57), BIG, 57), (V("tb", 57), -BIG, 39), (V("tc", 0, 32), -BIG, 32),
+    for o, x, n in ((V("s64"), BIG, 128), (V("M", C), -BIG, 32), (col("srow", 0), BIG, 1), (V("f1", 96), 0.0, 16),
+                    (V("tf", 0, 57), 0.0, 57), (V("tf", 57), 1.0, 39), (V("s64", 0, 128, 64), -BIG, 2),
+                    (V("tb", 0, 57), BIG, 57), (V("tb", 57), -BIG, 39), (V("tc", 0, 32), -BIG, 32),
                     (V("tc", 32), BIG, 96), (V("krow", C), 0.0, 8), (col("ksh", 0), 0.0, 1), (V("ksh", C + 1), 0.0, 7),
                     (V("pg", C), 32.0, 8), (col("eb", 0), float(-MID), 1), (V("z32"), 0.0, 32), (V("row", 0, 16), 0.0, 16),
                     (V("row", 16 + C), 0.0, 16), (V("tri", 16, 32), 1.0, 16), (V("tri", 64, 80), 1.0, 16)):
         fill(o, x, n)
     act(V("wt", 0, 16), V("j16", 0, 16), F.Sign, bias=col("cf", 0), scale=-1.0)
-    act(V("Mm", 88), V("hot", 8, 16), F.Identity, scale=-BIG)
+    act(col("Mm", 0), col("hot", 0), F.Identity, bias=-BIG, scale=2 * BIG)
+    act(V("Mn", 56), V("hot", 8, 16), F.Identity, scale=-BIG)
     for c, x in enumerate((-0.5, -16.5, -1.5)):
         act(col("rb", c), col("cf", 0), F.Identity, bias=x, scale=-1.0)
     for c in (32, 80):
@@ -313,54 +309,40 @@ def rank_program(g, core, T, topo):
     def quant_xa():
         quant(XA[0], XA[1], V("X", 0, 4 * CA))
 
-    def mm_sb():
-        mm(P(4, 0, nB), US[0], US[1], XB[0], XB[1])
-        mm(P(5, 0, nB), UK[0], UK[1], XB[0], XB[1])
-
-    def mm_sa():
-        mm(P(6, 0, CA), US[0], US[1], XA[0], XA[1])
-        mm(P(7, 0, CA), US[0], US[1], XA[0], XA[1])
-        mm(P(0, 0, CA), UK[0], UK[1], XA[0], XA[1])
-
-    def copy_sb():
-        act(V("srow", CA, C), P(4, 0, nB), F.Copy)
-
-    def copy_kb():
-        act(V("krow", CA, C), P(5, 0, nB), F.Copy)
-        act(V("ksh", CA + 1, C + 1), P(5, 0, nB), F.Copy)
-
-    def scan_mb():
-        scan(V("M", CA, C), V("s4", CA, C), V("srow", CA, C), -BIG, A.min, A.max)
+    def scan_mb(k):
+        if k == 0:
+            scan(V("M", CA, C), V("s4", CA, C), P(4, 0, nB), -BIG, A.min, A.max)
+        elif k == 1:
+            tt(V("Mn", 0, 56), V("M", CA + 3, C, 4), V("hot", 0, 56), A.mult)
+        else:
+            scan(V("pb"), V("s16", 0, 64), V("Mn"), 0.0, A.mult, A.add)
 
     def scan_ma():
+        tt(V("Mm", 1, CA), P(6, 1, CA), V("h4", 1, CA), A.min)
         scan(V("M", 1, CA), V("s4", 1, CA), P(6, 1, CA), BIG, A.min, A.max)
+        scan(V("p1"), V("s64"), V("Mm"), -BIG, A.min, A.max)
         act(V("srow", 1, CA), P(7, 1, CA), F.Copy)
 
     def plane(b):
         act(V("Xp", C * b, C * b + C), V("X", b, 4 * C, 4), F.Copy)
 
-    def unpack(t):
+    def unpack(t, first, bs):
         for b in range(4):
-            mm(P(4 + b, 0, C), V("eq", 128 * b, 128 * b + 128), V("es", 128 * b, 128 * b + 128), V("lq%d" % t), V("ls%d" % t))
-        for b in range(4):
-            act(V("Dp", C * b, C * b + C), P(4 + b, 0, C), F.Copy)
+            mm(P(first + b, 0, C), V("eq", 128 * b, 128 * b + 128), V("es", 128 * b, 128 * b + 128), V("lq%d" % t), V("ls%d" % t))
+        for b in bs:
+            act(V("Dp", C * b, C * b + C), P(first + b, 0, C), F.Copy)
 
     def sort(t):
         Mv = V("M", 3, C, 4)
-        tt(V("Mm", 0, 88), Mv, V("hot", 0, 88), A.mult)
-        scan(V("p1"), V("s16", 0, 96), V("Mm"), 0.0, A.mult, A.add)
-        for m in range(4):
-            ts(V("c1", 88 * m, 88 * m + 88), Mv, col("p1", 16 * m + 15), A.is_lt)
+        for m in (2, 3, 0, 1):
+            ts(V("c1", 88 * m, 88 * m + 88), Mv, col("p1", 64 * m + 63) if m < 2 else col("pb", 16 * m - 17), A.is_lt)
         for m in (4, 5):
-            act(V("sa", 128 * (m - 4), 128 * (m - 4) + 88), Mv, F.Sign, bias=col("p1", 16 * m + 15), scale=-1.0)
+            act(V("sa", 128 * (m - 4), 128 * (m - 4) + 88), Mv, F.Sign, bias=col("pb", 16 * m - 17), scale=-1.0)
         for m in (4, 5):
             act(V("sj", 128 * (m - 4), 128 * (m - 4) + 88), V("sa", 128 * (m - 4), 128 * (m - 4) + 88), F.Relu, acc=col("na", m))
-        act(V("krow", 0, CA), P(0, 0, CA), F.Copy)
-        act(V("ksh", 1, CA + 1), P(0, 0, CA), F.Copy)
+        act(V("srow", CA, C), P(4, 0, nB), F.Copy)
         if t == 0:
             late_constants()
-        else:
-            plane(0)
         scan(V("n1"), V("s88"), V("c1"), 0.0, A.min, A.add)
         cp(V("o1", 4, 6), V("na", 4, 6))
         cp(V("o1", 0, 4), V("n1", 87, 352, 88))
@@ -386,9 +368,11 @@ def rank_program(g, core, T, topo):
             act(V("sa", 128 * (m - 5), 128 * (m - 4)), V("cand"), F.Sign, bias=col("p2", 16 * m + 15), scale=-1.0)
         for m in (5, 6, 7):
             act(V("sj", 128 * (m - 5), 128 * (m - 4)), V("sa", 128 * (m - 5), 128 * (m - 4)), F.Relu, scale=-1.0, acc=col("nc", m))
-        plane(2)
+        act(V("krow", CA, C), P(5, 0, nB), F.Copy)
+        act(V("ksh", CA + 1, C + 1), P(5, 0, nB), F.Copy)
+        act(V("krow", 0, CA), P(0, 0, CA), F.Copy)
+        act(V("ksh", 1, CA + 1), P(0, 0, CA), F.Copy)
         if t == 0:
-            plane(0)
             ts(col("wl", 8), col("cf", 1), 272.0, A.mult, col("cf", 3), A.add)
         scan(V("n2"), V("s128"), V("c2"), 0.0, A.mult, A.add)
         cp(V("o2", 5, 8), V("nc", 5, 8))
@@ -403,6 +387,7 @@ def rank_program(g, core, T, topo):
         scan(back[0], back[1], back[1], 32.0, A.add, A.max)
         ts(V("ge", 0, MID), V("sg", 0, MID), 0.5, A.is_lt)
         scan(V("pp"), V("ge"), V("pg", 1, C + 1), 0.0, A.add, A.min)
+        plane(2)
         act(V("sg"), V("pp"), F.Sign, bias=col("rb", 2), acc=col("nd", 0))
         act(col("kb", 0), col("krow", 0), F.Copy)
         act(col("km", 0), col("krow", 0), F.Copy, scale=col("hot", 0))
@@ -426,13 +411,14 @@ def rank_program(g, core, T, topo):
         tt(V("m3"), V("c3"), V("wt"), A.mult)
         act(V("dd"), V("tn"), F.Identity, bias=1.0, scale=-2.0)
         plane(3)
+        plane(0)
         if t == 0:
             for b in range(4):
                 act(V("et", 512 * b + b, 512 * b + 512, 4), V("id"), F.Copy)
         if direct(t):
             if t == 0:
                 quant(V("eq"), V("es"), V("et"))
-            unpack(t)
+            unpack(t, 4, (0, 1, 2, 3))
         tt(V("t2"), V("lm"), V("tn"), A.mult)
         scan(V("n3"), V("s48"), V("m3"), 0.0, A.min, A.add)
         tt(V("ff"), V("t2"), V("eb", 0, 32), A.add)
@@ -445,6 +431,8 @@ def rank_program(g, core, T, topo):
         scan(V("row", 16, 16 + C), mw, V("dv"), 0.0, A.mult, A.add)
         tr(V("w1", 0, 96), V("row", 16, 112))
         tr(V("w1", 96), V("row", 0, 128))
+        tr(V("w2", 0, 256), V("row", 112, 368))
+        tr(V("w2", 256), V("row", 96, 384))
         ts(V("ob1"), IND(V("w1"), col("wl", 6)), float(MID), A.add)
 
     def pick(e, o, win, b, off):
@@ -469,9 +457,10 @@ def rank_program(g, core, T, topo):
         for b in range(4):
             act(rl(k, b), P(BANK[k] + b, 0, NEW[k]), F.Relu, scale=0.015625)
 
-    def add(k, b):
-        lo, hi = 4 * LO[k] + b, 4 * (LO[k] + NEW[k])
-        tt(V("X", lo, hi, 4), V("E", lo, hi, 4), rl(k, b), A.add)
+    def add(k, *bs):
+        for b in bs:
+            lo, hi = 4 * LO[k] + b, 4 * (LO[k] + NEW[k])
+            tt(V("X", lo, hi, 4), V("E", lo, hi, 4), rl(k, b), A.add)
 
     def swap(t):
         last = t == R - 1
@@ -479,19 +468,20 @@ def rank_program(g, core, T, topo):
         if not last:
             iota(V("mw", C * t + C, C * t + 2 * C), [[0, C]], 1, 0)
             iota(V("dw", C * t + C, C * t + 2 * C), [[0, C]], 0, 0)
-        tr(V("w2", 0, 256), V("row", 112, 368))
-        tr(V("w2", 256), V("row", 96, 384))
         ts(V("ob2"), IND(V("w2"), col("wl", 8)), float(MID), A.add)
         for k in (1, 2):
             for b in range(4):
                 pick("av"[b // 2], V("E", 4 * LO[k] + b, 4 * LO[k] + 512, 4), "Xp", b, V("ob2", 8 * k - 8, 8 * k))
             layer(k)
+        if last:
+            act(V("ob"), V("row", 16, 16 + C), F.Identity, bias=float(MID))
+            dma("s", T.ol[:], T.ob[0:128:16, :], [], [V("ob")])
         relu(1)
         relu(2)
 
         def border():
             for b in range(4):
-                pick("a" if direct(t) or b < 2 else "v", V("E", b, 4 * K, 4), "Dp", b, V("ll%d" % t))
+                pick("av"[b // 2], V("E", b, 4 * K, 4), "Dp", b, V("ll%d" % t))
 
         def scores_b():
             quant_xb()
@@ -501,42 +491,40 @@ def rank_program(g, core, T, topo):
                 act(V("yb", CA), P(4, 0, nB), F.Copy)
                 dma("s", T.y[:, CA:C], T.yb[:, CA:C], [], [V("yb", CA)])
             else:
-                mm_sb()
-                copy_sb()
-                copy_kb()
+                mm(P(4, 0, nB), US[0], US[1], XB[0], XB[1])
+                mm(P(5, 0, nB), UK[0], UK[1], XB[0], XB[1])
 
         if direct(t):
+            if t == 0:
+                quant(V("vq"), V("vs"), V("vt"))
+            add(1, 0, 1, 2, 3)
+            add(2, 0, 1)
             border()
-            for b in range(4):
-                add(1, b)
-            for b in range(3):
-                add(2, b)
+            add(2, 2)
             layer(0)
             relu(0)
             add(2, 3)
             scores_b()
+            add(0, 0, 1, 2, 3)
+            if not last:
+                scan_mb(0)
         else:
             add(1, 0)
             if t == 0:
                 quant(V("eq"), V("es"), V("et"))
-            unpack(t)
-            for k, b in ((1, 1), (1, 2), (1, 3), (2, 0), (2, 1), (2, 2), (2, 3)):
-                add(k, b)
-            scores_b()
-            if not last:
-                scan_mb()
+            unpack(t, 0, (0, 1, 2))
+            add(1, 1, 2, 3)
+            add(2, 0, 1, 2, 3)
             if t == 0:
                 quant(V("vq"), V("vs"), V("vt"))
+            scores_b()
+            cp(V("Dp", 3 * C), P(3, 0, C))
+            if not last:
+                scan_mb(0)
             border()
             layer(0)
             relu(0)
-        if direct(t) and t == 0:
-            quant(V("vq"), V("vs"), V("vt"))
-        if last:
-            act(V("ob"), V("row", 16, 16 + C), F.Identity, bias=float(MID))
-            dma("s", T.ol[:], T.ob[0:128:16, :], [], [V("ob")])
-        for b in range(4):
-            add(0, b)
+            add(0, 0, 1, 2, 3)
         quant_xa()
         if last:
             mm(P(6, 0, CA), V("vq"), V("vs"), XA[0], XA[1])
@@ -546,11 +534,13 @@ def rank_program(g, core, T, topo):
             cp(V("yb", 0, CA), P(6, 0, CA))
             dma("a", T.y[:, 0:CA], T.yb[:, 0:CA], [], [V("yb", 0, CA)])
         else:
-            mm_sa()
+            mm(P(6, 0, CA), US[0], US[1], XA[0], XA[1])
+            mm(P(7, 0, CA), US[0], US[1], XA[0], XA[1])
+            mm(P(0, 0, CA), UK[0], UK[1], XA[0], XA[1])
             ship(t + 1, 0)
             ship(t + 1, 1)
-            if direct(t):
-                scan_mb()
+            scan_mb(1)
+            scan_mb(2)
             scan_ma()
 
     pick_u(0)
@@ -567,12 +557,14 @@ def rank_program(g, core, T, topo):
     dma("s", T.wq[:].bitcast(dt.uint8), T.wc[:], [V("wq")], [])
     dma("s", T.wp[:], T.ws[:], [V("wp")], [])
     dma("s", T.vt[:], T.v[:], [V("vt")], [])
+    iota(V("iw"), [[1, 360]], -MID, 0)
+    iota(V("s48"), [[0, 2], [512, 48]], 0, 0)
     iota(V("mw", 0, C), [[0, C]], 1, 0)
     iota(V("dw", 0, C), [[0, C]], 0, 0)
-    copy_sb()
-    scan_mb()
+    scan_mb(0)
     scan_ma()
-    copy_kb()
+    scan_mb(1)
+    scan_mb(2)
     for t in range(R):
         sort(t)
         swap(t)

@@ -2,8 +2,10 @@ from concourse.mybir import dt, AluOpType as A, AxisListType, ActivationFunction
 
 C, K, R = 352, 96, 3
 CA = 128
+NB = C // 4
 BIG = 1e29
 MID = 176
+TW = 288
 Q, U8, F32, BF, I32, U16 = "float8_e4m3fn_x4", "uint8", "float32", "bfloat16", "int32", "uint16"
 
 
@@ -14,31 +16,31 @@ def _sb(n, d):
 SCRATCH = {
     "ps": ("psum", [128, 4096], F32),
     "X": _sb(4 * C, BF), "Xp": _sb(4 * C, BF), "E": _sb(4 * C, BF), "Dp": _sb(4 * C, BF),
-    "ut": _sb(512, BF), "vt": _sb(512, BF), "zt": _sb(C, BF), "et": _sb(2048, BF), "pj": _sb(128, F32), "id": _sb(128, BF),
+    "ut": _sb(512, BF), "vt": _sb(512, BF), "zt": _sb(C, BF), "et": _sb(2048, BF), "one": _sb(512, BF),
     "uq": _sb(128, Q), "us": _sb(128, U8), "u2q": _sb(256, Q), "u2s": _sb(256, U8),
     "vq": _sb(128, Q), "vs": _sb(128, U8), "wq": _sb(512, Q), "wp": _sb(512, U8),
     "eq": _sb(512, Q), "es": _sb(512, U8), "xq": _sb(C, Q), "xs": _sb(C, U8), "hq": _sb(384, Q), "hs": _sb(384, U8),
     "rq": _sb(C, Q), "rs": _sb(C, U8), "rl": _sb(6, U16),
     "Rl": _sb(1536, F32), "yb": _sb(C, F32), "ob": _sb(C, F32),
-    "srow": _sb(448, F32), "krow": _sb(360, F32), "ksh": _sb(360, F32),
+    "srow": _sb(448, F32), "krow": _sb(C, F32), "ksh": _sb(360, F32),
     "M": _sb(384, F32), "Mm": _sb(CA, F32), "p1": _sb(CA, F32), "h4": _sb(CA, F32), "s64": _sb(CA, F32),
     "Mn": _sb(64, F32), "pb": _sb(64, F32),
     "c1": _sb(352, BF), "n1": _sb(352, BF), "sa": _sb(384, BF), "sj": _sb(384, BF), "na": _sb(8, F32),
-    "o1": _sb(8, U16), "f1": _sb(112, BF), "q1": _sb(112, BF), "v1": _sb(96, F32), "t1": _sb(8, F32),
+    "o1": _sb(8, U16), "f1": _sb(96, BF), "q1": _sb(96, BF), "v1": _sb(96, F32), "t1": _sb(8, F32),
     "nb": _sb(8, F32), "oc4": _sb(8, U16), "cand": _sb(128, F32), "cm": _sb(128, F32), "p2": _sb(128, F32),
     "c2": _sb(640, BF), "n2": _sb(640, BF), "nc": _sb(8, F32), "o2": _sb(8, U16), "v2": _sb(128, F32),
     "gt": _sb(C, BF), "sg": _sb(C, BF), "ge": _sb(C, BF), "pg": _sb(C + 8, BF), "pp": _sb(C, BF),
     "le": _sb(C, BF), "lc": _sb(C, BF),
-    "nd": _sb(8, F32), "o3": _sb(2, U16), "kb": _sb(40, F32), "kl": _sb(32, F32), "km": _sb(40, F32),
-    "eb": _sb(40, F32), "p3": _sb(32, F32), "ln": _sb(32, F32), "lm": _sb(32, F32), "tn": _sb(32, F32),
-    "t2": _sb(32, F32), "ff": _sb(32, BF), "dd": _sb(32, BF), "c3": _sb(96, F32), "wt": _sb(96, F32),
-    "m3": _sb(96, F32), "n3": _sb(96, F32), "o4": _sb(2, U16), "dv": _sb(C, BF), "row": _sb(384, BF),
-    "w1": _sb(224, BF), "w2": _sb(544, BF), "ob1": _sb(16, U16), "ob2": _sb(16, U16),
+    "nd": _sb(8, F32), "o3": _sb(4, U16), "kb": _sb(32, F32), "kl": _sb(40, F32), "km": _sb(32, F32), "ke": _sb(32, F32),
+    "eb": _sb(40, F32), "p3": _sb(2, F32), "lm": _sb(32, F32), "tn": _sb(32, F32),
+    "t2": _sb(32, F32), "ff": _sb(32, BF), "dd": _sb(32, BF), "c3": _sb(96, F32), "wt": _sb(64, F32),
+    "m3": _sb(96, F32), "n3": _sb(2, F32), "o4": _sb(2, U16), "dv": _sb(C, BF), "row": _sb(384, BF),
+    "tw": _sb(3 * TW, BF), "ol0": _sb(16, U16), "ol1": _sb(16, U16), "ol2": _sb(16, U16),
     "mw": _sb(R * C, BF), "dw": _sb(R * C, BF), "z32": _sb(32, BF),
-    "ci": _sb(8, I32), "cf": _sb(16, F32), "pi": _sb(16, I32), "pl": _sb(16, U16), "j16": _sb(128, F32),
-    "hot": _sb(128, F32), "s16": _sb(128, F32), "s4": _sb(C, F32), "s88": _sb(352, BF), "s128": _sb(640, BF),
-    "s48": _sb(96, F32), "tf": _sb(96, BF), "tb": _sb(96, F32), "tc": _sb(128, F32), "iw": _sb(360, F32),
-    "tri": _sb(96, F32), "wl": _sb(10, U16), "wf": _sb(8, F32), "rb": _sb(4, F32),
+    "ci": _sb(8, I32), "cf": _sb(8, F32), "pi": _sb(16, F32), "pl": _sb(16, U16), "j16": _sb(128, F32), "j4": _sb(128, F32),
+    "hot": _sb(128, F32), "s16": _sb(128, F32), "s4": _sb(C, F32), "s88": _sb(176, BF), "s128": _sb(384, BF),
+    "tf": _sb(96, BF), "tb": _sb(96, F32), "tc": _sb(128, F32), "iw": _sb(360, F32),
+    "tri": _sb(32, F32), "wl": _sb(2, U16), "rb": _sb(4, F32), "src": _sb(128, F32),
 }
 for _t in range(R):
     SCRATCH["lq%d" % _t] = _sb(C, Q)
@@ -115,6 +117,9 @@ def rank_program(g, core, T, topo):
         for c in range(lo, hi, step):
             m |= 1 << c
         return (t[:, lo:hi:step] if step > 1 else t[:, lo:hi], name, m)
+
+    def back(name, lo, hi):
+        return (T[name][:, hi - 1:lo - 1:-1],) + V(name, lo, hi)[1:]
 
     def col(name, c):
         return V(name, c, c + 1)
@@ -222,7 +227,7 @@ def rank_program(g, core, T, topo):
 
     def ship(t, k):
         partner = cores[rank ^ (1 << t)]
-        src = (V("xq"), V("xs"), V("ob1", 0, 6))[k]
+        src = (V("xq"), V("xs"), V("ol0", 0, 6))[k]
         c = "qsl"[k]
         if direct(t):
             land, dst, sem = T["l" + c + str(t)][:], partner, "a" + c + str(t)
@@ -237,71 +242,20 @@ def rank_program(g, core, T, topo):
         note("far", acc, sent[-1], dict(clock["g"]))
         note("far", [V("l" + c + str(t))[1:] + (True,)], ("a" + c + str(t), counts(topo, cores, rank, t)[k]), {})
 
-    dma("s", T.ut[:], T.u[:], [V("ut")], [])
-    dma("a", T.X[:, 4 * CA:4 * C], T.x[:, 4 * CA:4 * C], [V("X", 4 * CA)], [])
-    dma("s", T.X[:, 0:4 * CA], T.x[:, 0:4 * CA], [V("X", 0, 4 * CA)], [])
-    iota(V("pi"), [[1, 2], [16, 8]], 0, 0, False)
-    iota(V("j16"), [[0, 8], [1, 16]], 0, 0)
-    iota(col("ci", 0), [[0, 1]], 0, 1, False)
-    iota(V("s88"), [[0, 4], [256, 88]], 0, 0)
-    iota(V("pj"), [[-1, 128]], 0, 1)
-    iota(V("wf", 0, 6), [[0, 3], [16, 2]], 0, 0)
-
     def fill(o, c, n):
-        act(o, V("j16", 0, n), F.Identity, bias=c, scale=0.0)
-
-    ms(V("et"), 0.0)
-    ts(col("ci", 1), col("ci", 0), 15, A.bitwise_and)
-    ts(col("ci", 2), col("ci", 0), 4, A.logical_shift_right)
-    cp(V("pl"), V("pi"))
-    ms(V("s128"), 1.0)
-    cp(col("cf", 0), col("ci", 1))
-    tt(col("ci", 3), col("ci", 0), col("ci", 2), A.add)
-    ms(V("zt"), 0.0)
-    ts(V("hot"), V("j16"), col("cf", 0), A.is_equal)
-    ts(col("ci", 4), col("ci", 3), 1, A.bitwise_and)
-    ms(V("s128", 0, 640, 128), 0.0)
-    ts(V("s16"), V("j16"), 0.5, A.is_gt)
-    cp(col("cf", 1), col("ci", 4))
-    ts(col("cf", 2), col("cf", 0), 5.0, A.min, 16.0, A.mult)
-    for b in range(4):
-        ts(V("h4", b, CA, 4), V("hot", 0, 32), 2 * BIG, A.mult, -BIG, A.add)
-    ts(V("id"), V("pj"), 0.0, A.is_equal)
-    for b in (1, 2, 3):
-        fill(V("s4", b, C, 4), BIG, 88)
-    fill(V("s4", 0, C, 4), -BIG, 88)
-    for o, x, n in ((V("s64"), BIG, 128), (V("M", C), -BIG, 32), (col("srow", 0), BIG, 1), (V("f1", 96), 0.0, 16),
-                    (V("tf", 0, 57), 0.0, 57), (V("tf", 57), 1.0, 39), (V("s64", 0, 128, 64), -BIG, 2),
-                    (V("tb", 0, 57), BIG, 57), (V("tb", 57), -BIG, 39), (V("tc", 0, 32), -BIG, 32),
-                    (V("tc", 32), BIG, 96), (V("krow", C), 0.0, 8), (col("ksh", 0), 0.0, 1), (V("ksh", C + 1), 0.0, 7),
-                    (V("pg", C), 32.0, 8), (col("eb", 0), float(-MID), 1), (V("z32"), 0.0, 32), (V("row", 0, 16), 0.0, 16),
-                    (V("row", 16 + C), 0.0, 16), (V("tri", 16, 32), 1.0, 16), (V("tri", 64, 80), 1.0, 16)):
-        fill(o, x, n)
-    act(V("wt", 0, 16), V("j16", 0, 16), F.Sign, bias=col("cf", 0), scale=-1.0)
-    act(col("Mm", 0), col("hot", 0), F.Identity, bias=-BIG, scale=2 * BIG)
-    act(V("Mn", 56), V("hot", 8, 16), F.Identity, scale=-BIG)
-    for c, x in enumerate((-0.5, -16.5, -1.5)):
-        act(col("rb", c), col("cf", 0), F.Identity, bias=x, scale=-1.0)
-    for c in (32, 80):
-        act(V("tri", c, c + 16), V("wt", 0, 16), F.Relu)
-    quant(V("uq"), V("us"), V("ut"))
-
-    def pick_u(k):
-        o, l = V("u2q", 128 * k, 128 * k + 128), V("pl", 8 * k, 8 * k + 8)
-        op("v", lambda: g.vector.tensor_copy(o[0].bitcast(dt.uint32), T.uq[:].bitcast(dt.uint32).indirect(l[0])), [o], [V("uq"), l])
-        act(V("u2s", 128 * k, 128 * k + 128), IND(V("us"), l), F.Copy)
-
-    def late_constants():
-        act(col("rb", 3), col("cf", 0), F.Identity, bias=17.5)
-        act(col("cf", 3), col("cf", 0), F.Identity, scale=16.0)
-        for c in (0, 48):
-            act(V("tri", c, c + 16), V("tri", c + 32, c + 48), F.Identity, bias=1.0, scale=-1.0)
+        act(o, V("src", 0, n), F.Identity, bias=c, scale=0.0)
 
     XB = (V("xq", CA), V("xs", CA))
     XA = (V("xq", 0, CA), V("xs", 0, CA))
     US = (V("u2q", 0, 128), V("u2s", 0, 128))
     UK = (V("u2q", 128), V("u2s", 128))
     nB = C - CA
+    hot = lambda lo, hi: V("hot", lo, hi)
+
+    def pick_u(k):
+        o, l = V("u2q", 128 * k, 128 * k + 128), V("pl", 8 * k, 8 * k + 8)
+        op("v", lambda: g.vector.tensor_copy(o[0].bitcast(dt.uint32), T.uq[:].bitcast(dt.uint32).indirect(l[0])), [o], [V("uq"), l])
+        act(V("u2s", 128 * k, 128 * k + 128), IND(V("us"), l), F.Copy)
 
     def quant_xb():
         quant(XB[0], XB[1], V("X", 4 * CA))
@@ -313,136 +267,156 @@ def rank_program(g, core, T, topo):
         if k == 0:
             scan(V("M", CA, C), V("s4", CA, C), P(4, 0, nB), -BIG, A.min, A.max)
         elif k == 1:
-            tt(V("Mn", 0, 56), V("M", CA + 3, C, 4), V("hot", 0, 56), A.mult)
+            tt(V("Mn", 0, 56), V("M", CA + 3, C, 4), hot(0, 56), A.mult)
         else:
             scan(V("pb"), V("s16", 0, 64), V("Mn"), 0.0, A.mult, A.add)
-
-    def scan_ma():
-        tt(V("Mm", 1, CA), P(6, 1, CA), V("h4", 1, CA), A.min)
-        scan(V("M", 1, CA), V("s4", 1, CA), P(6, 1, CA), BIG, A.min, A.max)
-        scan(V("p1"), V("s64"), V("Mm"), -BIG, A.min, A.max)
-        act(V("srow", 1, CA), P(7, 1, CA), F.Copy)
 
     def plane(b):
         act(V("Xp", C * b, C * b + C), V("X", b, 4 * C, 4), F.Copy)
 
-    def unpack(t, first, bs):
+    def unpack(t):
         for b in range(4):
-            mm(P(first + b, 0, C), V("eq", 128 * b, 128 * b + 128), V("es", 128 * b, 128 * b + 128), V("lq%d" % t), V("ls%d" % t))
-        for b in bs:
-            act(V("Dp", C * b, C * b + C), P(first + b, 0, C), F.Copy)
+            mm(P(4 + b, 0, C), V("eq", 128 * b, 128 * b + 128), V("es", 128 * b, 128 * b + 128), V("lq%d" % t), V("ls%d" % t))
 
-    def sort(t):
+    def unpacked(b):
+        act(V("Dp", C * b, C * b + C), P(4 + b, 0, C), F.Copy)
+
+    def sort(t, spare):
+        def gap():
+            if spare:
+                spare.pop(0)()
+
         Mv = V("M", 3, C, 4)
-        for m in (2, 3, 0, 1):
-            ts(V("c1", 88 * m, 88 * m + 88), Mv, col("p1", 64 * m + 63) if m < 2 else col("pb", 16 * m - 17), A.is_lt)
+        tt(V("Mm", 1, CA), P(6, 1, CA), V("h4", 1, CA), A.add)
+        scan(V("M", 1, CA), V("s4", 1, CA), P(6, 1, CA), BIG, A.min, A.max)
+        act(V("srow", 1, CA), P(7, 1, CA), F.Copy)
+        if t == 0:
+            scan_mb(1)
+        scan(V("p1"), V("s64"), V("Mm"), -BIG, A.min, A.max)
+        if t == 0:
+            scan_mb(2)
+        for m in (2, 3, 0, 1) if t else (0, 1, 2, 3):
+            ts(V("c1", NB * m, NB * m + NB), Mv, col("p1", 64 * m + 63) if m < 2 else col("pb", 16 * m - 17), A.is_lt)
         for m in (4, 5):
-            act(V("sa", 128 * (m - 4), 128 * (m - 4) + 88), Mv, F.Sign, bias=col("pb", 16 * m - 17), scale=-1.0)
+            act(V("sa", 128 * (m - 4), 128 * (m - 4) + NB), Mv, F.Sign, bias=col("pb", 16 * m - 17), scale=-1.0)
         for m in (4, 5):
-            act(V("sj", 128 * (m - 4), 128 * (m - 4) + 88), V("sa", 128 * (m - 4), 128 * (m - 4) + 88), F.Relu, acc=col("na", m))
+            act(V("sj", 128 * (m - 4), 128 * (m - 4) + NB), V("sa", 128 * (m - 4), 128 * (m - 4) + NB), F.Relu, acc=col("na", m))
         act(V("srow", CA, C), P(4, 0, nB), F.Copy)
-        if t == 0:
-            late_constants()
-        scan(V("n1"), V("s88"), V("c1"), 0.0, A.min, A.add)
-        cp(V("o1", 4, 6), V("na", 4, 6))
-        cp(V("o1", 0, 4), V("n1", 87, 352, 88))
-        cp(V("f1", 0, 96), IND(V("tf"), V("o1", 0, 6)))
-        scan(V("q1", 0, 110), V("f1", 0, 110), V("f1", 0, 110), 0.0, A.add, A.max)
-        for m in range(2):
-            act(V("sj", 128 * m, 128 * m + 110), V("q1", 0, 110), F.Sign, bias=col("rb", m), acc=col("nb", m))
-        plane(1)
+        plane(0)
+        halves = (1, 0) if t else (0, 1)
+        for h in halves:
+            scan(V("n1", 2 * NB * h, 2 * NB * (h + 1)), V("s88"), V("c1", 2 * NB * h, 2 * NB * (h + 1)), 0.0, A.min, A.add)
+        for h in (halves[0], 2, halves[1]):
+            cp(V("o1", 2 * h, 2 * h + 2), V("n1", (2 * h + 1) * NB - 1, (2 * h + 2) * NB, NB) if h < 2 else V("na", 4, 6))
+        for lo, hi in ((2, 6), (0, 2)) if t else ((0, 2), (2, 6)):
+            cp(V("f1", 16 * lo, 16 * hi), IND(V("tf"), V("o1", lo, hi)))
         tt(V("v1"), IND(V("tb"), V("o1", 0, 6)), V("M", 3, 384, 4), A.min)
-        scan(V("srow", C), V("v1"), V("v1"), -BIG, A.max, A.max)
+        scan(V("q1", 0, NB), V("f1", 0, NB), V("f1", 0, NB), 0.0, A.add, A.max)
+        for m in range(2):
+            act(V("sj", 128 * m, 128 * m + NB), V("q1", 0, NB), F.Sign, bias=col("rb", m), acc=col("nb", m))
+        scan(back("srow", C, 448), V("v1"), V("v1"), -BIG, A.max, A.max)
+        gap()
         for b in range(4):
-            ts(V("oc4", 2 * b, 2 * b + 2), V("nb", 0, 2), -2.0, A.mult, float(220 + b), A.add)
-        act(V("cand"), IND(V("srow"), V("oc4")), F.Copy)
-        tt(V("cm"), IND(V("srow"), V("oc4")), V("hot"), A.mult)
-        if t == 0:
-            ts(V("wl", 0, 6), V("wf", 0, 6), col("cf", 0), A.add)
-        scan(V("p2"), V("s16"), V("cm"), 0.0, A.mult, A.add)
-        if t == 0:
-            ts(col("wl", 6), col("cf", 1), 112.0, A.mult, col("cf", 2), A.add)
-        for m in range(5):
-            ts(V("c2", 128 * m, 128 * m + 128), V("cand"), col("p2", 16 * m + 15), A.is_gt)
-        for m in (5, 6, 7):
-            act(V("sa", 128 * (m - 5), 128 * (m - 4)), V("cand"), F.Sign, bias=col("p2", 16 * m + 15), scale=-1.0)
-        for m in (5, 6, 7):
-            act(V("sj", 128 * (m - 5), 128 * (m - 4)), V("sa", 128 * (m - 5), 128 * (m - 4)), F.Relu, scale=-1.0, acc=col("nc", m))
-        act(V("krow", CA, C), P(5, 0, nB), F.Copy)
+            ts(V("oc4", 2 * b, 2 * b + 2), V("nb", 0, 2), -2.0, A.mult, float(2 * NB + b), A.add)
+        for h in range(2):
+            l = V("oc4", 4 * h, 4 * h + 4)
+            act(V("cand", 64 * h, 64 * h + 64), IND(V("srow"), l), F.Copy)
+            tt(V("cm", 64 * h, 64 * h + 64), IND(V("srow"), l), hot(0, 64), A.mult)
+        for h in range(2):
+            scan(V("p2", 64 * h, 64 * h + 64), V("s16", 0, 64), V("cm", 64 * h, 64 * h + 64), 0.0, A.mult, A.add)
+        for m in range(3):
+            act(V("sa", 128 * m, 128 * m + 128), V("cand"), F.Sign, bias=col("p2", 16 * m + 15), scale=-1.0)
+        for m in range(3):
+            act(V("sj", 128 * m, 128 * m + 128), V("sa", 128 * m, 128 * m + 128), F.Relu, scale=-1.0, acc=col("nc", m))
+        for m in range(3, 8):
+            ts(V("c2", 128 * m - 384, 128 * m - 256), V("cand"), col("p2", 16 * m + 15), A.is_gt)
+        act(V("krow", CA), P(5, 0, nB), F.Copy)
         act(V("ksh", CA + 1, C + 1), P(5, 0, nB), F.Copy)
         act(V("krow", 0, CA), P(0, 0, CA), F.Copy)
         act(V("ksh", 1, CA + 1), P(0, 0, CA), F.Copy)
-        if t == 0:
-            ts(col("wl", 8), col("cf", 1), 272.0, A.mult, col("cf", 3), A.add)
-        scan(V("n2"), V("s128"), V("c2"), 0.0, A.mult, A.add)
-        cp(V("o2", 5, 8), V("nc", 5, 8))
-        cp(V("o2", 0, 5), V("n2", 127, 640, 128))
-        tt(V("v2"), IND(V("tc"), V("o2")), V("cand"), A.max)
+        act(col("kl", 32), col("krow", C - 1), F.Copy)
+        scan(V("n2", 0, 384), V("s128"), V("c2", 0, 384), 0.0, A.mult, A.add)
+        scan(V("n2", 384), V("s128", 0, 256), V("c2", 384), 0.0, A.mult, A.add)
+        cp(V("o2", 0, 3), V("nc", 0, 3))
+        cp(V("o2", 3, 6), V("n2", 127, 384, 128))
+        cp(V("o2", 6, 8), V("n2", 511, 640, 128))
+        tt(V("v2", 0, 96), IND(V("tc"), V("o2", 0, 6)), V("cand", 0, 96), A.max)
+        tt(V("v2", 96), IND(V("tc"), V("o2", 6, 8)), V("cand", 96), A.max)
+        gap()
         red(col("t1", 0), V("v2"), A.min)
-        S = V("srow", 0, C)
-        ts(V("gt"), S, col("t1", 0), A.is_gt, -1.0, A.mult)
-        act(V("sg"), S, F.Sign, bias=col("t1", 0), scale=-1.0)
+        gap()
+        ts(V("gt"), V("srow", 0, C), col("t1", 0), A.is_gt, -1.0, A.mult)
+        act(V("sg", MID), V("srow", MID, C), F.Sign, bias=col("t1", 0), scale=-1.0)
         act(V("ge", MID), V("sg", MID), F.Sign, bias=1.0, scale=-1.0)
-        back = [(T[n][:, C - 1:0:-1],) + V(n, 1, C)[1:] for n in ("pg", "gt")]
-        scan(back[0], back[1], back[1], 32.0, A.add, A.max)
-        ts(V("ge", 0, MID), V("sg", 0, MID), 0.5, A.is_lt)
+        plane(1)
+        ts(V("ge", 0, MID), V("srow", 0, MID), col("t1", 0), A.is_ge)
+        scan(back("pg", 1, C), back("gt", 1, C), back("gt", 1, C), 32.0, A.add, A.max)
+        gap()
         scan(V("pp"), V("ge"), V("pg", 1, C + 1), 0.0, A.add, A.min)
-        plane(2)
-        act(V("sg"), V("pp"), F.Sign, bias=col("rb", 2), acc=col("nd", 0))
-        act(col("kb", 0), col("krow", 0), F.Copy)
-        act(col("km", 0), col("krow", 0), F.Copy, scale=col("hot", 0))
-        ts(V("le"), V("pp"), col("rb", 3), A.is_le)
-        scan(V("lc"), V("le"), V("zt"), float(-MID), A.add, A.add)
-        ts(col("o3", 0), col("nd", 0), -0.5, A.mult, 176.0, A.add)
-        ts(col("o3", 1), col("lc", C - 1), float(MID), A.add)
-        tt(V("km", 1, 33), IND(V("krow"), V("o3")), V("hot", 1, 33), A.mult)
-        act(V("eb", 1, 33), IND(V("iw"), V("o3")), F.Copy)
-        act(V("kb", 1, 33), IND(V("krow"), V("o3")), F.Copy)
-        act(V("kl"), IND(V("ksh"), V("o3")), F.Copy)
-        scan(V("p3"), V("s16", 0, 32), V("km", 0, 32), 0.0, A.mult, A.add)
-        tt(V("ln"), V("eb", 1, 33), V("eb", 0, 32), A.subtract)
-        act(V("lm"), V("ln"), F.Identity, bias=-1.0)
-        ts(V("c3", 0, 32), V("kb", 0, 32), col("p3", 15), A.is_gt)
-        tt(V("wt"), IND(V("ln"), V("wl", 0, 6)), V("tri"), A.mult)
-        ts(V("c3", 32, 48), V("kb", 0, 16), col("p3", 15), A.is_ge)
-        ts(V("c3", 48, 64), V("kb", 16, 32), col("p3", 31), A.is_gt)
-        ts(V("c3", 64, 96), V("kb", 0, 32), col("p3", 31), A.is_ge)
-        tt(V("tn"), V("kb", 0, 32), V("kl"), A.is_lt)
-        tt(V("m3"), V("c3"), V("wt"), A.mult)
+        gap()
+        act(V("sg", 0, C - 16), V("pp", 0, C - 16), F.Sign, bias=col("rb", 0), acc=col("nd", 0))
+        ts(V("le", 16), V("pp", 16), col("rb", 2), A.is_le)
+        gap()
+        scan(V("lc", 16), V("le", 16), V("zt", 16), float(16 - MID), A.add, A.add)
+        ts(col("o3", 0), col("nd", 0), -0.5, A.mult, float(C - 16) / 2, A.add)
+        ts(col("o3", 2), col("lc", C - 1), float(MID), A.add)
+        L = (col("o3", 0), col("o3", 2))
+        for n, w, h in (("eb", "iw", 0), ("kb", "krow", 0), ("eb", "iw", 1), ("kb", "krow", 1), ("kl", "ksh", 0), ("kl", "ksh", 1)):
+            act(V(n, 16 * h, 16 * h + 16), IND(V(w), L[h]), F.Copy)
+        for h in range(2):
+            tt(V("km", 16 * h, 16 * h + 16), IND(V("krow"), L[h]), hot(0, 16), A.mult)
+            tt(V("ke", 16 * h, 16 * h + 16), IND(V("krow"), L[h]), V("tri", 16 * h, 16 * h + 16), A.add)
+        for h in range(2):
+            red(col("p3", h), V("km", 16 * h, 16 * h + 16), A.add)
+        tt(V("wt", 16, 48), V("eb", 1, 33), V("eb", 0, 32), A.subtract)
+        tt(V("wt", 0, 16), V("eb", 1, 17), V("eb", 0, 16), A.subtract)
+        tt(V("wt", 48), V("eb", 16, 32), V("eb", 17, 33), A.subtract)
+        act(V("lm"), V("wt", 16, 48), F.Identity, bias=-1.0)
+        ts(V("c3", 0, 16), V("ke", 0, 16), col("p3", 0), A.is_equal)
+        ts(V("c3", 16, 48), V("kb"), col("p3", 0), A.is_gt)
+        ts(V("c3", 48, 80), V("kb"), col("p3", 1), A.is_ge)
+        ts(V("c3", 80), V("ke", 16), col("p3", 1), A.is_equal)
+        tt(V("tn"), V("kb"), V("kl", 1, 33), A.is_lt)
         act(V("dd"), V("tn"), F.Identity, bias=1.0, scale=-2.0)
+        unpack(t)
+        plane(2)
         plane(3)
-        plane(0)
-        if t == 0:
-            for b in range(4):
-                act(V("et", 512 * b + b, 512 * b + 512, 4), V("id"), F.Copy)
-        if direct(t):
-            if t == 0:
-                quant(V("eq"), V("es"), V("et"))
-            unpack(t, 4, (0, 1, 2, 3))
+        for b in range(4):
+            unpacked(b)
+        for h in range(2):
+            tt(V("m3", 48 * h, 48 * h + 48), V("c3", 48 * h, 48 * h + 48), V("wt", 16 * h, 16 * h + 48), A.mult)
         tt(V("t2"), V("lm"), V("tn"), A.mult)
-        scan(V("n3"), V("s48"), V("m3"), 0.0, A.min, A.add)
+        for h in range(2):
+            red(col("n3", h), V("m3", 48 * h, 48 * h + 48), A.add)
         tt(V("ff"), V("t2"), V("eb", 0, 32), A.add)
-        cp(V("o4"), V("n3", 47, 96, 48))
+        cp(V("o4"), V("n3"))
+        gap()
         mw, dw = V("mw", C * t, C * t + C), V("dw", C * t, C * t + C)
         cp(IND(mw, V("o4")), V("z32"))
         cp(IND(dw, V("o4")), V("dd"))
+        gap()
         scan(V("dv"), mw, dw, 0.0, A.mult, A.add)
+        gap()
         cp(IND(V("dv"), V("o4")), V("ff"))
+        gap()
         scan(V("row", 16, 16 + C), mw, V("dv"), 0.0, A.mult, A.add)
-        tr(V("w1", 0, 96), V("row", 16, 112))
-        tr(V("w1", 96), V("row", 0, 128))
-        tr(V("w2", 0, 256), V("row", 112, 368))
-        tr(V("w2", 256), V("row", 96, 384))
-        ts(V("ob1"), IND(V("w1"), col("wl", 6)), float(MID), A.add)
+        while spare:
+            gap()
+        for k in (1, 0, 2):
+            tr(V("tw", TW * k, TW * k + 128), V("row", 16 + LO[k], 144 + LO[k]))
+            tr(V("tw", TW * k + 128, TW * k + TW), V("row", LO[k], 160 + LO[k]))
+        for k in (1, 0, 2):
+            ts(V("ol%d" % k), IND(V("tw", TW * k, TW * k + TW), col("wl", 0)), float(MID), A.add)
 
-    def pick(e, o, win, b, off):
-        src = IND(V(win, C * b, C * b + C), off)
+    LO, NEW, BANK = (0, K, K + 128), (K, 128, 128), (0, 0, 4)
+
+    def pick(e, t, k, b):
+        o = V("E", 4 * LO[k] + b, 4 * (LO[k] + NEW[k]), 4)
+        src = IND(V("Xp" if k else "Dp", C * b, C * b + C), V("ol%d" % k, 0, 8) if k else V("ll%d" % t))
         if e == "v":
             cp(o, src)
         else:
             act(o, src, F.Copy)
-
-    LO, NEW, BANK = (0, K, K + 128), (K, 128, 128), (0, 0, 4)
 
     def layer(k):
         q, s = V("hq", 128 * k, 128 * k + 128), V("hs", 128 * k, 128 * k + 128)
@@ -453,8 +427,8 @@ def rank_program(g, core, T, topo):
     def rl(k, b):
         return V("Rl", 512 * k + 128 * b, 512 * k + 128 * b + NEW[k])
 
-    def relu(k):
-        for b in range(4):
+    def relu(k, *bs):
+        for b in bs:
             act(rl(k, b), P(BANK[k] + b, 0, NEW[k]), F.Relu, scale=0.015625)
 
     def add(k, *bs):
@@ -465,68 +439,55 @@ def rank_program(g, core, T, topo):
     def swap(t):
         last = t == R - 1
         ship(t, 2)
-        if not last:
-            iota(V("mw", C * t + C, C * t + 2 * C), [[0, C]], 1, 0)
-            iota(V("dw", C * t + C, C * t + 2 * C), [[0, C]], 0, 0)
-        ts(V("ob2"), IND(V("w2"), col("wl", 8)), float(MID), A.add)
-        for k in (1, 2):
-            for b in range(4):
-                pick("av"[b // 2], V("E", 4 * LO[k] + b, 4 * LO[k] + 512, 4), "Xp", b, V("ob2", 8 * k - 8, 8 * k))
-            layer(k)
-        if last:
-            act(V("ob"), V("row", 16, 16 + C), F.Identity, bias=float(MID))
-            dma("s", T.ol[:], T.ob[0:128:16, :], [], [V("ob")])
-        relu(1)
-        relu(2)
-
-        def border():
-            for b in range(4):
-                pick("av"[b // 2], V("E", b, 4 * K, 4), "Dp", b, V("ll%d" % t))
+        for e, k, b in (("v", 1, 2), ("a", 1, 0), ("v", 1, 3), ("a", 1, 1), ("v", 2, 3), ("a", 2, 0), ("a", 2, 1)):
+            pick(e, t, k, b)
+        layer(1)
+        pick("v", t, 2, 2)
+        layer(2)
+        relu(1, 0, 1, 2, 3)
 
         def scores_b():
-            quant_xb()
+            for k in (1, 2):
+                quant(V("xq", LO[k], LO[k] + 128), V("xs", LO[k], LO[k] + 128), V("X", 4 * LO[k], 4 * LO[k] + 512))
             if last:
                 mm(P(4, 0, nB), V("vq"), V("vs"), XB[0], XB[1])
                 dma("s", T.oc[:, 4 * CA:4 * C], T.xq[:, CA:C].bitcast(dt.uint8), [], [XB[0]])
-                act(V("yb", CA), P(4, 0, nB), F.Copy)
-                dma("s", T.y[:, CA:C], T.yb[:, CA:C], [], [V("yb", CA)])
             else:
                 mm(P(4, 0, nB), US[0], US[1], XB[0], XB[1])
                 mm(P(5, 0, nB), UK[0], UK[1], XB[0], XB[1])
 
         if direct(t):
-            if t == 0:
-                quant(V("vq"), V("vs"), V("vt"))
+            relu(2, 0, 1)
+            pick("a", t, 0, 0)
+            pick("a", t, 0, 1)
+            relu(2, 2, 3)
+            pick("a", t, 0, 2)
+            if last:
+                act(V("ob"), V("row", 16, 16 + C), F.Identity, bias=float(MID))
+                dma("s", T.ol[:], T.ob[0:128:16, :], [], [V("ob")])
             add(1, 0, 1, 2, 3)
-            add(2, 0, 1)
-            border()
-            add(2, 2)
+            add(2, 0)
+            pick("v", t, 0, 3)
+            add(2, 1)
             layer(0)
-            relu(0)
-            add(2, 3)
+            relu(0, 0, 1, 2, 3)
+            add(2, 2, 3)
             scores_b()
             add(0, 0, 1, 2, 3)
-            if not last:
-                scan_mb(0)
         else:
-            add(1, 0)
-            if t == 0:
-                quant(V("eq"), V("es"), V("et"))
-            unpack(t, 0, (0, 1, 2))
-            add(1, 1, 2, 3)
+            relu(2, 0, 1, 2, 3)
+            add(1, 0, 1, 2, 3)
             add(2, 0, 1, 2, 3)
-            if t == 0:
-                quant(V("vq"), V("vs"), V("vt"))
-            scores_b()
-            cp(V("Dp", 3 * C), P(3, 0, C))
-            if not last:
-                scan_mb(0)
-            border()
+            for b in range(4):
+                pick("a", t, 0, b)
             layer(0)
-            relu(0)
+            relu(0, 0, 1, 2, 3)
+            scores_b()
             add(0, 0, 1, 2, 3)
-        quant_xa()
         if last:
+            act(V("yb", CA), P(4, 0, nB), F.Copy)
+            dma("s", T.y[:, CA:C], T.yb[:, CA:C], [], [V("yb", CA)])
+            quant_xa()
             mm(P(6, 0, CA), V("vq"), V("vs"), XA[0], XA[1])
             dma("s", T.oc[:, 0:4 * CA], T.xq[:, 0:CA].bitcast(dt.uint8), [], [XA[0]])
             for k in range(4):
@@ -534,6 +495,8 @@ def rank_program(g, core, T, topo):
             cp(V("yb", 0, CA), P(6, 0, CA))
             dma("a", T.y[:, 0:CA], T.yb[:, 0:CA], [], [V("yb", 0, CA)])
         else:
+            scan_mb(0)
+            quant_xa()
             mm(P(6, 0, CA), US[0], US[1], XA[0], XA[1])
             mm(P(7, 0, CA), US[0], US[1], XA[0], XA[1])
             mm(P(0, 0, CA), UK[0], UK[1], XA[0], XA[1])
@@ -541,8 +504,48 @@ def rank_program(g, core, T, topo):
             ship(t + 1, 1)
             scan_mb(1)
             scan_mb(2)
-            scan_ma()
 
+    dma("s", T.ut[:], T.u[:], [V("ut")], [])
+    dma("a", T.X[:, 4 * CA:4 * C], T.x[:, 4 * CA:4 * C], [V("X", 4 * CA)], [])
+    dma("s", T.X[:, 0:4 * CA], T.x[:, 0:4 * CA], [V("X", 0, 4 * CA)], [])
+    iota(V("pi"), [[1, 2], [16, 8]], 0, 0)
+    iota(col("ci", 0), [[0, 1]], 0, 1, False)
+    iota(V("j16"), [[0, 8], [1, 16]], 0, 0)
+    iota(V("j4"), [[0, 2], [1, 16], [0, 4]], 0, 0)
+    iota(V("s88"), [[0, 2], [256, NB]], 0, 0)
+    iota(V("iw"), [[1, 360]], -MID, 0)
+    ms(V("src"), 0.0)
+    ms(V("s128"), 1.0)
+    ms(V("zt"), 0.0)
+    cp(V("pl"), V("pi"))
+    ts(col("ci", 1), col("ci", 0), 15, A.bitwise_and)
+    ts(col("ci", 2), col("ci", 0), 4, A.logical_shift_right)
+    ms(V("s128", 0, 384, 128), 0.0)
+    for o, x in ((V("tf", 0, 57), 0.0), (V("tf", 57), 1.0)):
+        ms(o, x)
+    cp(col("cf", 0), col("ci", 1))
+    tt(col("ci", 3), col("ci", 0), col("ci", 2), A.add)
+    for o, x in ((V("tb", 0, 57), BIG), (V("tb", 57), -BIG)):
+        ms(o, x)
+    ts(V("hot"), V("j16"), col("cf", 0), A.is_equal)
+    ts(col("ci", 4), col("ci", 3), 1, A.bitwise_and)
+    ts(V("h4"), V("j4"), col("cf", 0), A.not_equal, -BIG, A.mult)
+    for b in (1, 2, 3):
+        fill(V("s4", b, C, 4), BIG, NB)
+    fill(V("s4", 0, C, 4), -BIG, NB)
+    for o, x, n in ((V("s64"), BIG, 128), (V("M", C), -BIG, 32), (col("srow", 0), BIG, 1), (V("tc", 0, 32), -BIG, 32),
+                    (V("s64", 0, 128, 64), -BIG, 2), (V("tc", 32), BIG, 96), (col("ksh", 0), 0.0, 1), (V("ksh", C + 1), 0.0, 7),
+                    (V("pg", C), 32.0, 8), (col("eb", 32), float(C - MID), 1), (V("z32"), 0.0, 32),
+                    (V("row", 0, 16), 0.0, 16), (V("row", 16 + C), 0.0, 16)):
+        fill(o, x, n)
+    act(V("s16"), V("j16"), F.Sign)
+    act(col("Mm", 0), col("hot", 0), F.Identity, bias=-BIG, scale=2 * BIG)
+    act(V("Mn", 56), hot(8, 16), F.Identity, scale=-BIG)
+    for c, x, s in ((0, -0.5, -1.0), (1, -16.5, -1.0), (2, 16.0, 1.0)):
+        act(col("rb", c), col("cf", 0), F.Identity, bias=x, scale=s)
+    quant(V("uq"), V("us"), V("ut"))
+    cp(col("cf", 1), col("ci", 4))
+    ts(col("cf", 2), col("cf", 0), 7.0, A.min, 16.0, A.mult)
     pick_u(0)
     quant_xb()
     mm(P(4, 0, nB), US[0], US[1], XB[0], XB[1])
@@ -554,19 +557,24 @@ def rank_program(g, core, T, topo):
     pick_u(1)
     mm(P(5, 0, nB), UK[0], UK[1], XB[0], XB[1])
     mm(P(0, 0, CA), UK[0], UK[1], XA[0], XA[1])
-    dma("s", T.wq[:].bitcast(dt.uint8), T.wc[:], [V("wq")], [])
+    dma("s", T.wq[:].bitcast(dt.uint8), T.wc[:], [V("wq")], [col("X", 0), col("X", 4 * CA)])
     dma("s", T.wp[:], T.ws[:], [V("wp")], [])
     dma("s", T.vt[:], T.v[:], [V("vt")], [])
-    iota(V("iw"), [[1, 360]], -MID, 0)
-    iota(V("s48"), [[0, 2], [512, 48]], 0, 0)
-    iota(V("mw", 0, C), [[0, C]], 1, 0)
-    iota(V("dw", 0, C), [[0, C]], 0, 0)
-    scan_mb(0)
-    scan_ma()
-    scan_mb(1)
-    scan_mb(2)
+    iota(V("one"), [[0, 512]], 1, 0)
+    for b in range(4):
+        o = V("et", 512 * b, 512 * b + 512)
+        op("g", lambda: g.affine_select(o[0], T.one[:], [[1, 512]], A.is_equal, 0.0, -b, -4), [o], [V("one")])
     for t in range(R):
-        sort(t)
+        iota(V("mw", C * t, C * t + C), [[0, C]], 1, 0)
+        iota(V("dw", C * t, C * t + C), [[0, C]], 0, 0)
+    scan_mb(0)
+    first = [lambda: ts(V("tri", 0, 16), V("j16", 0, 16), col("cf", 0), A.is_ge, -BIG, A.mult),
+             lambda: ts(V("tri", 16), V("j16", 0, 16), col("cf", 0), A.is_lt, -BIG, A.mult)]
+    first += [lambda b=b: quant(V("eq", 128 * b, 128 * b + 128), V("es", 128 * b, 128 * b + 128), V("et", 512 * b, 512 * b + 512))
+              for b in range(4)]
+    first += [lambda: ts(col("wl", 0), col("cf", 1), float(TW // 2), A.mult, col("cf", 2), A.add)]
+    for t in range(R):
+        sort(t, first if t == 0 else [lambda: quant(V("vq"), V("vs"), V("vt"))] if t == 1 else [])
         swap(t)
     for s, n in sent:
         g.wait_ge(T.sem[s], n)

@@ -5,7 +5,7 @@ CA = 128
 NB = C // 4
 BIG = 1e29
 MID = 176
-TW = 288
+RW = C + 16
 Q, U8, F32, BF, I32, U16 = "float8_e4m3fn_x4", "uint8", "float32", "bfloat16", "int32", "uint16"
 
 
@@ -15,13 +15,13 @@ def _sb(n, d):
 
 SCRATCH = {
     "ps": ("psum", [128, 4096], F32),
-    "X": _sb(4 * C, BF), "Xp": _sb(4 * C, BF), "E": _sb(4 * C, BF), "Dp": _sb(4 * C, BF),
-    "ut": _sb(512, BF), "vt": _sb(512, BF), "zt": _sb(C, BF), "et": _sb(2048, BF), "one": _sb(512, BF),
+    "X": _sb(4 * C, BF), "Xp": _sb(8 * C, BF), "E": _sb(4 * C, BF), "Dp": _sb(8 * C, BF),
+    "ut": _sb(512, BF), "vt": _sb(512, BF), "zt": _sb(C, BF), "et0": _sb(514, BF), "et1": _sb(514, BF), "one": _sb(514, BF),
     "uq": _sb(128, Q), "us": _sb(128, U8), "u2q": _sb(256, Q), "u2s": _sb(256, U8),
     "vq": _sb(128, Q), "vs": _sb(128, U8), "wq": _sb(512, Q), "wp": _sb(512, U8),
     "eq": _sb(512, Q), "es": _sb(512, U8), "xq": _sb(C, Q), "xs": _sb(C, U8), "hq": _sb(384, Q), "hs": _sb(384, U8),
     "rq": _sb(C, Q), "rs": _sb(C, U8), "rl": _sb(6, U16),
-    "Rl": _sb(1536, F32), "yb": _sb(C, F32), "ob": _sb(C, F32),
+    "Rl": _sb(1536, F32), "yb": _sb(C, F32), "ob": _sb(RW, F32),
     "srow": _sb(448, F32), "krow": _sb(C, F32), "ksh": _sb(360, F32),
     "M": _sb(384, F32), "Mm": _sb(CA, F32), "p1": _sb(CA, F32), "h4": _sb(CA, F32), "s64": _sb(CA, F32),
     "Mn": _sb(64, F32), "pb": _sb(64, F32),
@@ -32,15 +32,15 @@ SCRATCH = {
     "gt": _sb(C, BF), "sg": _sb(C, BF), "ge": _sb(C, BF), "pg": _sb(C + 8, BF), "pp": _sb(C, BF),
     "le": _sb(C, BF), "lc": _sb(C, BF),
     "nd": _sb(8, F32), "o3": _sb(4, U16), "kb": _sb(32, F32), "kl": _sb(40, F32), "km": _sb(32, F32), "ke": _sb(32, F32),
-    "eb": _sb(40, F32), "p3": _sb(2, F32), "lm": _sb(32, F32), "tn": _sb(32, F32),
-    "t2": _sb(32, F32), "ff": _sb(32, BF), "dd": _sb(32, BF), "c3": _sb(96, F32), "wt": _sb(64, F32),
-    "m3": _sb(96, F32), "n3": _sb(2, F32), "o4": _sb(2, U16), "dv": _sb(C, BF), "row": _sb(384, BF),
-    "tw": _sb(3 * TW, BF), "ol0": _sb(16, U16), "ol1": _sb(16, U16), "ol2": _sb(16, U16),
-    "mw": _sb(R * C, BF), "dw": _sb(R * C, BF), "z32": _sb(32, BF),
+    "eb": _sb(40, F32), "p3": _sb(2, F32), "hl": _sb(32, F32), "lm": _sb(32, F32), "tn": _sb(32, F32),
+    "t2": _sb(32, F32), "ff": _sb(32, F32), "c3": _sb(96, F32), "wt": _sb(64, F32),
+    "m3": _sb(96, F32), "n3": _sb(2, F32), "o4": _sb(2, U16), "row": _sb(RW, F32),
+    "tw": _sb(3 * 256, F32), "ol0": _sb(16, U16), "ol1": _sb(16, U16), "ol2": _sb(16, U16),
+    "mw": _sb(2 * R * RW, F32), "z32": _sb(32, F32),
     "ci": _sb(8, I32), "cf": _sb(8, F32), "pi": _sb(16, F32), "pl": _sb(16, U16), "j16": _sb(128, F32), "j4": _sb(128, F32),
     "hot": _sb(128, F32), "s16": _sb(128, F32), "s4": _sb(C, F32), "s88": _sb(176, BF), "s128": _sb(384, BF),
     "tf": _sb(96, BF), "tb": _sb(96, F32), "tc": _sb(128, F32), "iw": _sb(360, F32),
-    "tri": _sb(32, F32), "wl": _sb(2, U16), "rb": _sb(4, F32), "src": _sb(128, F32),
+    "tri": _sb(32, F32), "wl": _sb(2, U16), "rb": _sb(4, F32), "b4": _sb(4, F32), "el": _sb(40, F32), "src": _sb(128, F32),
 }
 for _t in range(R):
     SCRATCH["lq%d" % _t] = _sb(C, Q)
@@ -272,14 +272,28 @@ def rank_program(g, core, T, topo):
             scan(V("pb"), V("s16", 0, 64), V("Mn"), 0.0, A.mult, A.add)
 
     def plane(b):
-        act(V("Xp", C * b, C * b + C), V("X", b, 4 * C, 4), F.Copy)
+        act(V("Xp", C * (2 * b + 1), C * (2 * b + 2)), V("X", b, 4 * C, 4), F.Copy)
+
+    def mirror(b):
+        o, i = back("Xp", 2 * C * b + 1, 2 * C * b + C), V("X", 4 + b, 4 * C, 4)
+        op("g", lambda: g.affine_select(o[0], i[0], [[0, C - 1]], A.is_ge, 0.0, 0, 0), [o], [i])
+
+    def marks(t):
+        iota(V("mw", 2 * RW * t, 2 * RW * (t + 1)), [[0, 2 * RW]], 1, 0)
 
     def unpack(t):
         for b in range(4):
             mm(P(4 + b, 0, C), V("eq", 128 * b, 128 * b + 128), V("es", 128 * b, 128 * b + 128), V("lq%d" % t), V("ls%d" % t))
 
     def unpacked(b):
-        act(V("Dp", C * b, C * b + C), P(4 + b, 0, C), F.Copy)
+        act(V("Dp", C * (2 * b + 1), C * (2 * b + 2)), P(4 + b, 0, C), F.Copy)
+        act(back("Dp", 2 * C * b + 1, 2 * C * b + C), P(4 + b, 1, C), F.Copy)
+
+    def turn(k, h):
+        tr(V("tw", 256 * k + 128 * h, 256 * k + 128 * h + NEW[k]), V("row", LO[k] + 16 * h, LO[k] + 16 * h + NEW[k]))
+
+    def listed(k):
+        ts(V("ol%d" % k), IND(V("tw", 256 * k, 256 * k + 256), col("wl", 0)), float(C), A.add)
 
     def sort(t, spare):
         def gap():
@@ -303,6 +317,7 @@ def rank_program(g, core, T, topo):
             act(V("sj", 128 * (m - 4), 128 * (m - 4) + NB), V("sa", 128 * (m - 4), 128 * (m - 4) + NB), F.Relu, acc=col("na", m))
         act(V("srow", CA, C), P(4, 0, nB), F.Copy)
         plane(0)
+        plane(1)
         halves = (1, 0) if t else (0, 1)
         for h in halves:
             scan(V("n1", 2 * NB * h, 2 * NB * (h + 1)), V("s88"), V("c1", 2 * NB * h, 2 * NB * (h + 1)), 0.0, A.min, A.add)
@@ -316,8 +331,8 @@ def rank_program(g, core, T, topo):
             act(V("sj", 128 * m, 128 * m + NB), V("q1", 0, NB), F.Sign, bias=col("rb", m), acc=col("nb", m))
         scan(back("srow", C, 448), V("v1"), V("v1"), -BIG, A.max, A.max)
         gap()
-        for b in range(4):
-            ts(V("oc4", 2 * b, 2 * b + 2), V("nb", 0, 2), -2.0, A.mult, float(2 * NB + b), A.add)
+        for m in range(2):
+            ts(V("oc4", 4 * m, 4 * m + 4), V("b4"), col("nb", m), A.subtract, 2.0, A.mult)
         for h in range(2):
             l = V("oc4", 4 * h, 4 * h + 4)
             act(V("cand", 64 * h, 64 * h + 64), IND(V("srow"), l), F.Copy)
@@ -335,6 +350,7 @@ def rank_program(g, core, T, topo):
         act(V("krow", 0, CA), P(0, 0, CA), F.Copy)
         act(V("ksh", 1, CA + 1), P(0, 0, CA), F.Copy)
         act(col("kl", 32), col("krow", C - 1), F.Copy)
+        plane(2)
         scan(V("n2", 0, 384), V("s128"), V("c2", 0, 384), 0.0, A.mult, A.add)
         scan(V("n2", 384), V("s128", 0, 256), V("c2", 384), 0.0, A.mult, A.add)
         cp(V("o2", 0, 3), V("nc", 0, 3))
@@ -348,7 +364,7 @@ def rank_program(g, core, T, topo):
         ts(V("gt"), V("srow", 0, C), col("t1", 0), A.is_gt, -1.0, A.mult)
         act(V("sg", MID), V("srow", MID, C), F.Sign, bias=col("t1", 0), scale=-1.0)
         act(V("ge", MID), V("sg", MID), F.Sign, bias=1.0, scale=-1.0)
-        plane(1)
+        plane(3)
         ts(V("ge", 0, MID), V("srow", 0, MID), col("t1", 0), A.is_ge)
         scan(back("pg", 1, C), back("gt", 1, C), back("gt", 1, C), 32.0, A.add, A.max)
         gap()
@@ -366,53 +382,51 @@ def rank_program(g, core, T, topo):
         for h in range(2):
             tt(V("km", 16 * h, 16 * h + 16), IND(V("krow"), L[h]), hot(0, 16), A.mult)
             tt(V("ke", 16 * h, 16 * h + 16), IND(V("krow"), L[h]), V("tri", 16 * h, 16 * h + 16), A.add)
-        for h in range(2):
-            red(col("p3", h), V("km", 16 * h, 16 * h + 16), A.add)
+        red(col("p3", 0), V("km", 0, 16), A.add)
+        tt(V("wt", 0, 15), V("eb", 1, 16), V("eb", 0, 15), A.subtract)
+        red(col("p3", 1), V("km", 16), A.add)
         tt(V("wt", 16, 48), V("eb", 1, 33), V("eb", 0, 32), A.subtract)
-        tt(V("wt", 0, 16), V("eb", 1, 17), V("eb", 0, 16), A.subtract)
         tt(V("wt", 48), V("eb", 16, 32), V("eb", 17, 33), A.subtract)
-        act(V("lm"), V("wt", 16, 48), F.Identity, bias=-1.0)
         ts(V("c3", 0, 16), V("ke", 0, 16), col("p3", 0), A.is_equal)
         ts(V("c3", 16, 48), V("kb"), col("p3", 0), A.is_gt)
         ts(V("c3", 48, 80), V("kb"), col("p3", 1), A.is_ge)
         ts(V("c3", 80), V("ke", 16), col("p3", 1), A.is_equal)
-        tt(V("tn"), V("kb"), V("kl", 1, 33), A.is_lt)
-        act(V("dd"), V("tn"), F.Identity, bias=1.0, scale=-2.0)
+        for h in range(2):
+            act(V("el", 16 * h, 16 * h + 16), IND(V("iw"), L[h]), F.Identity, bias=-1.0)
         unpack(t)
-        plane(2)
-        plane(3)
         for b in range(4):
             unpacked(b)
+        tt(V("tn"), V("kb"), V("kl", 1, 33), A.is_lt)
         for h in range(2):
             tt(V("m3", 48 * h, 48 * h + 48), V("c3", 48 * h, 48 * h + 48), V("wt", 16 * h, 16 * h + 48), A.mult)
-        tt(V("t2"), V("lm"), V("tn"), A.mult)
+        tt(V("hl"), V("eb", 0, 32), V("el", 1, 33), A.add)
         for h in range(2):
             red(col("n3", h), V("m3", 48 * h, 48 * h + 48), A.add)
-        tt(V("ff"), V("t2"), V("eb", 0, 32), A.add)
-        cp(V("o4"), V("n3"))
+        tt(V("t2"), V("hl"), V("tn"), A.mult)
         gap()
-        mw, dw = V("mw", C * t, C * t + C), V("dw", C * t, C * t + C)
-        cp(IND(mw, V("o4")), V("z32"))
-        cp(IND(dw, V("o4")), V("dd"))
-        gap()
-        scan(V("dv"), mw, dw, 0.0, A.mult, A.add)
-        gap()
-        cp(IND(V("dv"), V("o4")), V("ff"))
-        gap()
-        scan(V("row", 16, 16 + C), mw, V("dv"), 0.0, A.mult, A.add)
+        ts(V("o4"), V("n3"), col("cf", 3), A.add)
+        tt(V("ff"), V("eb", 0, 32), V("t2"), A.subtract)
+        mw, dw = 2 * RW * t, 2 * RW * t + RW
+        cp(IND(V("mw", mw, mw + RW), V("o4")), V("z32"))
+        cp(IND(V("mw", dw, dw + RW), V("o4")), V("ff"))
         while spare:
             gap()
-        for k in (1, 0, 2):
-            tr(V("tw", TW * k, TW * k + 128), V("row", 16 + LO[k], 144 + LO[k]))
-            tr(V("tw", TW * k + 128, TW * k + TW), V("row", LO[k], 160 + LO[k]))
-        for k in (1, 0, 2):
-            ts(V("ol%d" % k), IND(V("tw", TW * k, TW * k + TW), col("wl", 0)), float(MID), A.add)
+        scan(V("row"), V("mw", mw, mw + RW), V("mw", dw, dw + RW), 0.0, A.mult, A.add)
+        a, b = (1, 0) if direct(t) else (0, 1)
+        for k in (a, b):
+            turn(k, 0)
+            turn(k, 1)
+        listed(a)
+        turn(2, 0)
+        listed(b)
+        turn(2, 1)
+        ship(t, 2)
 
     LO, NEW, BANK = (0, K, K + 128), (K, 128, 128), (0, 0, 4)
 
     def pick(e, t, k, b):
         o = V("E", 4 * LO[k] + b, 4 * (LO[k] + NEW[k]), 4)
-        src = IND(V("Xp" if k else "Dp", C * b, C * b + C), V("ol%d" % k, 0, 8) if k else V("ll%d" % t))
+        src = IND(V("Xp" if k else "Dp", 2 * C * b, 2 * C * (b + 1)), V("ol%d" % k, 0, 8) if k else V("ll%d" % t))
         if e == "v":
             cp(o, src)
         else:
@@ -438,13 +452,27 @@ def rank_program(g, core, T, topo):
 
     def swap(t):
         last = t == R - 1
-        ship(t, 2)
-        for e, k, b in (("v", 1, 2), ("a", 1, 0), ("v", 1, 3), ("a", 1, 1), ("v", 2, 3), ("a", 2, 0), ("a", 2, 1)):
-            pick(e, t, k, b)
-        layer(1)
+        pick("a", t, 1, 0)
+        pick("a", t, 1, 1)
+        pick("v", t, 1, 2)
+        listed(2)
+        if not last:
+            marks(t + 1)
+        pick("v", t, 1, 3)
+        pick("a", t, 2, 0)
+        pick("a", t, 2, 1)
         pick("v", t, 2, 2)
+        layer(1)
+        pick("v", t, 2, 3)
         layer(2)
         relu(1, 0, 1, 2, 3)
+        add(1, 0)
+
+        def places():
+            if last:
+                act(V("ob"), V("row"), F.Abs)
+                for h in range(2):
+                    dma("s", T.ol[h:8:2, :], T.ob[16 * h:128:32, 16 * h:16 * h + C], [], [V("ob")])
 
         def scores_b():
             for k in (1, 2):
@@ -462,10 +490,8 @@ def rank_program(g, core, T, topo):
             pick("a", t, 0, 1)
             relu(2, 2, 3)
             pick("a", t, 0, 2)
-            if last:
-                act(V("ob"), V("row", 16, 16 + C), F.Identity, bias=float(MID))
-                dma("s", T.ol[:], T.ob[0:128:16, :], [], [V("ob")])
-            add(1, 0, 1, 2, 3)
+            places()
+            add(1, 1, 2, 3)
             add(2, 0)
             pick("v", t, 0, 3)
             add(2, 1)
@@ -476,12 +502,14 @@ def rank_program(g, core, T, topo):
             add(0, 0, 1, 2, 3)
         else:
             relu(2, 0, 1, 2, 3)
-            add(1, 0, 1, 2, 3)
-            add(2, 0, 1, 2, 3)
+            places()
+            add(1, 1, 2, 3)
+            add(2, 0, 1)
             for b in range(4):
-                pick("a", t, 0, b)
+                pick("av"[b // 2], t, 0, b)
             layer(0)
             relu(0, 0, 1, 2, 3)
+            add(2, 2, 3)
             scores_b()
             add(0, 0, 1, 2, 3)
         if last:
@@ -502,50 +530,54 @@ def rank_program(g, core, T, topo):
             mm(P(0, 0, CA), UK[0], UK[1], XA[0], XA[1])
             ship(t + 1, 0)
             ship(t + 1, 1)
+            for b in range(4):
+                mirror(b)
             scan_mb(1)
             scan_mb(2)
 
     dma("s", T.ut[:], T.u[:], [V("ut")], [])
-    dma("a", T.X[:, 4 * CA:4 * C], T.x[:, 4 * CA:4 * C], [V("X", 4 * CA)], [])
+    dma("s", T.X[:, 4 * CA:4 * C], T.x[:, 4 * CA:4 * C], [V("X", 4 * CA)], [])
     dma("s", T.X[:, 0:4 * CA], T.x[:, 0:4 * CA], [V("X", 0, 4 * CA)], [])
     iota(V("pi"), [[1, 2], [16, 8]], 0, 0)
     iota(col("ci", 0), [[0, 1]], 0, 1, False)
     iota(V("j16"), [[0, 8], [1, 16]], 0, 0)
     iota(V("j4"), [[0, 2], [1, 16], [0, 4]], 0, 0)
     iota(V("s88"), [[0, 2], [256, NB]], 0, 0)
-    iota(V("iw"), [[1, 360]], -MID, 0)
     ms(V("src"), 0.0)
-    ms(V("s128"), 1.0)
-    ms(V("zt"), 0.0)
+    ms(V("one"), 1.0)
     cp(V("pl"), V("pi"))
-    ts(col("ci", 1), col("ci", 0), 15, A.bitwise_and)
-    ts(col("ci", 2), col("ci", 0), 4, A.logical_shift_right)
-    ms(V("s128", 0, 384, 128), 0.0)
+    for c, m in enumerate((15, 1, 6, 16)):
+        ts(col("ci", c + 1), col("ci", 0), m, A.bitwise_and)
     for o, x in ((V("tf", 0, 57), 0.0), (V("tf", 57), 1.0)):
         ms(o, x)
-    cp(col("cf", 0), col("ci", 1))
-    tt(col("ci", 3), col("ci", 0), col("ci", 2), A.add)
+    cp(V("cf", 0, 4), V("ci", 1, 5))
     for o, x in ((V("tb", 0, 57), BIG), (V("tb", 57), -BIG)):
         ms(o, x)
     ts(V("hot"), V("j16"), col("cf", 0), A.is_equal)
-    ts(col("ci", 4), col("ci", 3), 1, A.bitwise_and)
     ts(V("h4"), V("j4"), col("cf", 0), A.not_equal, -BIG, A.mult)
+
+    def unit(h):
+        o = V("et%d" % h)
+        op("g", lambda: g.affine_select(o[0], T.one[:], [[1, 514]], A.is_equal, 0.0, -2 - h, -4), [o], [V("one")])
+
+    def quant_e(b):
+        lo = 2 - b // 2 * 2
+        quant(V("eq", 128 * b, 128 * b + 128), V("es", 128 * b, 128 * b + 128), V("et%d" % (b % 2), lo, lo + 512))
+
+    unit(0)
     for b in (1, 2, 3):
         fill(V("s4", b, C, 4), BIG, NB)
     fill(V("s4", 0, C, 4), -BIG, NB)
     for o, x, n in ((V("s64"), BIG, 128), (V("M", C), -BIG, 32), (col("srow", 0), BIG, 1), (V("tc", 0, 32), -BIG, 32),
                     (V("s64", 0, 128, 64), -BIG, 2), (V("tc", 32), BIG, 96), (col("ksh", 0), 0.0, 1), (V("ksh", C + 1), 0.0, 7),
-                    (V("pg", C), 32.0, 8), (col("eb", 32), float(C - MID), 1), (V("z32"), 0.0, 32),
-                    (V("row", 0, 16), 0.0, 16), (V("row", 16 + C), 0.0, 16)):
+                    (V("pg", C), 32.0, 8), (col("eb", 32), float(C), 1), (col("el", 32), float(C - 1), 1), (V("z32"), 0.0, 32),
+                    (col("wt", 15), 0.0, 1)):
         fill(o, x, n)
     act(V("s16"), V("j16"), F.Sign)
     act(col("Mm", 0), col("hot", 0), F.Identity, bias=-BIG, scale=2 * BIG)
     act(V("Mn", 56), hot(8, 16), F.Identity, scale=-BIG)
-    for c, x, s in ((0, -0.5, -1.0), (1, -16.5, -1.0), (2, 16.0, 1.0)):
-        act(col("rb", c), col("cf", 0), F.Identity, bias=x, scale=s)
     quant(V("uq"), V("us"), V("ut"))
-    cp(col("cf", 1), col("ci", 4))
-    ts(col("cf", 2), col("cf", 0), 7.0, A.min, 16.0, A.mult)
+    ms(V("s128"), 1.0)
     pick_u(0)
     quant_xb()
     mm(P(4, 0, nB), US[0], US[1], XB[0], XB[1])
@@ -557,22 +589,30 @@ def rank_program(g, core, T, topo):
     pick_u(1)
     mm(P(5, 0, nB), UK[0], UK[1], XB[0], XB[1])
     mm(P(0, 0, CA), UK[0], UK[1], XA[0], XA[1])
+    act(V("b4"), V("j16", 0, 4), F.Identity, bias=float(NB), scale=0.5)
+    for c, x, s in ((0, -0.5, -1.0), (1, -16.5, -1.0), (2, 16.0, 1.0)):
+        act(col("rb", c), col("cf", 0), F.Identity, bias=x, scale=s)
+    for o, n in ((V("tw", K, 128), 32), (V("tw", 128 + K, 256), 32), (V("Xp", 0, 8 * C, 2 * C), 4), (V("Dp", 0, 8 * C, 2 * C), 4)):
+        fill(o, 0.0, n)
     dma("s", T.wq[:].bitcast(dt.uint8), T.wc[:], [V("wq")], [col("X", 0), col("X", 4 * CA)])
     dma("s", T.wp[:], T.ws[:], [V("wp")], [])
     dma("s", T.vt[:], T.v[:], [V("vt")], [])
-    iota(V("one"), [[0, 512]], 1, 0)
+    unit(1)
+    iota(V("iw"), [[1, 360]], 0, 0)
+    marks(0)
     for b in range(4):
-        o = V("et", 512 * b, 512 * b + 512)
-        op("g", lambda: g.affine_select(o[0], T.one[:], [[1, 512]], A.is_equal, 0.0, -b, -4), [o], [V("one")])
-    for t in range(R):
-        iota(V("mw", C * t, C * t + C), [[0, C]], 1, 0)
-        iota(V("dw", C * t, C * t + C), [[0, C]], 0, 0)
+        mirror(b)
+    ms(V("s128", 0, 384, 128), 0.0)
     scan_mb(0)
-    first = [lambda: ts(V("tri", 0, 16), V("j16", 0, 16), col("cf", 0), A.is_ge, -BIG, A.mult),
-             lambda: ts(V("tri", 16), V("j16", 0, 16), col("cf", 0), A.is_lt, -BIG, A.mult)]
-    first += [lambda b=b: quant(V("eq", 128 * b, 128 * b + 128), V("es", 128 * b, 128 * b + 128), V("et", 512 * b, 512 * b + 512))
-              for b in range(4)]
-    first += [lambda: ts(col("wl", 0), col("cf", 1), float(TW // 2), A.mult, col("cf", 2), A.add)]
+
+    def small():
+        ms(V("zt"), 0.0)
+        ts(V("tri", 0, 16), V("j16", 0, 16), col("cf", 0), A.is_ge, -BIG, A.mult)
+        ts(V("tri", 16), V("j16", 0, 16), col("cf", 0), A.is_lt, -BIG, A.mult)
+
+    first = [small, lambda: ts(col("cf", 4), col("cf", 1), 128.0, A.mult, col("cf", 3), A.add)]
+    first += [lambda b=b: quant_e(b) for b in range(4)]
+    first += [lambda: ts(col("wl", 0), col("cf", 2), 16.0, A.mult, col("cf", 4), A.add)]
     for t in range(R):
         sort(t, first if t == 0 else [lambda: quant(V("vq"), V("vs"), V("vt"))] if t == 1 else [])
         swap(t)

from concourse.mybir import dt, AluOpType as A, AxisListType, ActivationFunctionType as F

C, K, R = 352, 96, 3
CA = 128
NB = C // 4
BIG = 1e29
MID = 176
RW = C + 16
Q, U8, F32, BF, I32, U16 = "float8_e4m3fn_x4", "uint8", "float32", "bfloat16", "int32", "uint16"


def _sb(n, d):
    return ("sbuf", [128, n], d)


SCRATCH = {
    "ps": ("psum", [128, 4096], F32),
    "X": _sb(4 * C, BF), "Xp": _sb(8 * C, BF), "E": _sb(4 * C, BF), "Dp": _sb(8 * C, BF),
    "ut": _sb(512, BF), "vt": _sb(512, BF), "zt": _sb(C, BF), "et0": _sb(514, BF), "et1": _sb(514, BF), "one": _sb(514, BF),
    "uq": _sb(128, Q), "us": _sb(128, U8), "u2q": _sb(256, Q), "u2s": _sb(256, U8),
    "vq": _sb(128, Q), "vs": _sb(128, U8), "wq": _sb(512, Q), "wp": _sb(512, U8),
    "eq": _sb(512, Q), "es": _sb(512, U8), "xq": _sb(C, Q), "xs": _sb(C, U8), "hq": _sb(384, Q), "hs": _sb(384, U8),
    "rq": _sb(C, Q), "rs": _sb(C, U8), "rl": _sb(6, U16),
    "Rl": _sb(1536, F32), "yb": _sb(C, F32), "ob": _sb(RW, F32),
    "srow": _sb(448, F32), "krow": _sb(C, F32), "ksh": _sb(360, F32),
    "M": _sb(384, F32), "Mm": _sb(CA, F32), "p1": _sb(CA, F32), "h4": _sb(CA, F32), "s64": _sb(CA, F32),
    "Mn": _sb(64, F32), "pb": _sb(64, F32),
    "c1": _sb(352, BF), "n1": _sb(352, BF), "sa": _sb(384, BF), "sj": _sb(384, BF), "na": _sb(8, F32),
    "o1": _sb(8, U16), "f1": _sb(96, BF), "q1": _sb(96, BF), "v1": _sb(96, F32), "t1": _sb(8, F32),
    "nb": _sb(8, F32), "oc4": _sb(8, U16), "cand": _sb(128, F32), "cm": _sb(128, F32), "p2": _sb(128, F32),
    "c2": _sb(640, BF), "n2": _sb(640, BF), "nc": _sb(8, F32), "o2": _sb(8, U16), "v2": _sb(128, F32),
    "gt": _sb(C, BF), "sg": _sb(C, BF), "ge": _sb(C, BF), "pg": _sb(C + 8, BF), "pp": _sb(C, BF),
    "le": _sb(C, BF), "lc": _sb(C, BF),
    "nd": _sb(8, F32), "o3": _sb(4, U16), "kb": _sb(32, F32), "kl": _sb(40, F32), "km": _sb(32, F32), "ke": _sb(32, F32),
    "eb": _sb(40, F32), "p3": _sb(2, F32), "hl": _sb(32, F32), "lm": _sb(32, F32), "tn": _sb(32, F32),
    "t2": _sb(32, F32), "ff": _sb(32, F32), "c3": _sb(96, F32), "wt": _sb(64, F32),
    "m3": _sb(96, F32), "n3": _sb(2, F32), "o4": _sb(2, U16), "row": _sb(RW, F32),
    "tw": _sb(3 * 256, F32), "ol0": _sb(16, U16), "ol1": _sb(16, U16), "ol2": _sb(16, U16),
    "mw": _sb(2 * R * RW, F32), "z32": _sb(32, F32),
    "ci": _sb(8, I32), "cf": _sb(8, F32), "pi": _sb(16, F32), "pl": _sb(16, U16), "j16": _sb(128, F32), "j4": _sb(128, F32),
    "hot": _sb(128, F32), "s16": _sb(128, F32), "s4": _sb(C, F32), "s88": _sb(176, BF), "s128": _sb(384, BF),
    "tf": _sb(96, BF), "tb": _sb(96, F32), "tc": _sb(128, F32), "iw": _sb(360, F32),
    "tri": _sb(32, F32), "wl": _sb(2, U16), "rb": _sb(4, F32), "b4": _sb(4, F32), "el": _sb(40, F32), "src": _sb(128, F32),
}
for _t in range(R):
    SCRATCH["lq%d" % _t] = _sb(C, Q)
    SCRATCH["ls%d" % _t] = _sb(C, U8)
    SCRATCH["ll%d" % _t] = _sb(6, U16)
SEMAPHORES = (["cv", "ca", "ct", "cg", "sent", "hq", "hs", "hl"]
              + [n + str(t) for n in ("aq", "as", "al", "sq", "ss", "sl") for t in range(R)] + ["d%d" % i for i in range(24)])


def bits(engines):
    return sum(1 << e for e in engines)


def helpers(topo, src, dst):
    h = [c for c in topo.cores_of(src) if c != src and topo.may_write(c, dst)]
    return sorted(h, key=lambda c: topo.die(c) != topo.die(src))[:2]


def counts(topo, cores, r, t):
    p = r ^ (1 << t)
    if topo.may_write(cores[p], cores[r]):
        n = len(topo.engines(cores[p], cores[r]))
        return n, n, n
    h = helpers(topo, cores[p], cores[r])
    n = len(topo.engines(h[1], cores[r]))
    return len(topo.engines(h[0], cores[r])), n, n


def hand_on(g, core, T, topo):
    cores = T.cores
    for t in range(R):
        for r in range(len(cores)):
            src, dst = cores[r], cores[r ^ (1 << t)]
            if topo.may_write(src, dst):
                continue
            h = helpers(topo, src, dst)
            if core not in h:
                continue
            n = len(topo.engines(src, core))
            rid, pid = topo.addr(dst, core)
            e = topo.engines(core, dst)
            if core == h[0]:
                g.wait_ge(T.sem.hq, n)
                g.remote_dma(T["lq%d" % t][:].bitcast(dt.uint8), T.rq[:].bitcast(dt.uint8), T.sem["aq%d" % t], T.sem.sent, pid, rid, bits(e))
                g.wait_ge(T.sem.sent, len(e))
            else:
                g.wait_ge(T.sem.hs, n)
                g.remote_dma(T["ls%d" % t][:], T.rs[:], T.sem["as%d" % t], T.sem.sent, pid, rid, bits(e))
                g.wait_ge(T.sem.hl, n)
                g.remote_dma(T["ll%d" % t][:], T.rl[:], T.sem["al%d" % t], T.sem.sent, pid, rid, bits(e))
                g.wait_ge(T.sem.sent, 2 * len(e))


def rank_program(g, core, T, topo):
    rank = T.rank_of(core)
    if rank is None:
        hand_on(g, core, T, topo)
        return
    cores = T.cores
    queue = {"v": g.vector, "a": g.scalar, "t": g.tensor, "g": g, "s": g.sync}
    csem = {"v": "cv", "a": "ca", "t": "ct", "g": "cg"}
    done = {k: 0 for k in csem}
    clock = {k: {} for k in queue}
    past = {}
    dmas = []
    sent = []
    seqno = [0]

    def V(name, lo=0, hi=None, step=1):
        t = T[name]
        if hi is None:
            hi = t.shape[1]
        m = 0
        for c in range(lo, hi, step):
            m |= 1 << c
        return (t[:, lo:hi:step] if step > 1 else t[:, lo:hi], name, m)

    def back(name, lo, hi):
        return (T[name][:, hi - 1:lo - 1:-1],) + V(name, lo, hi)[1:]

    def col(name, c):
        return V(name, c, c + 1)

    def P(bank, lo, hi):
        return (T.ps[:, 512 * bank + lo:512 * bank + hi], "ps", 1 << bank)

    def IND(win, off):
        return (win[0].indirect(off[0]), win[1], win[2], off)

    def order(e, outs, ins):
        acc = [(v[1], v[2], True) for v in outs] + [(v[1], v[2], False) for v in ins]
        acc += [(v[3][1], v[3][2], False) for v in list(outs) + list(ins) if len(v) > 3]
        need = []
        for name, m, w in acc:
            for (m2, w2, e2, ev, ck, seq) in past.get(name, []):
                if m & m2 and (w or w2 or (name == "ps" and e2 != e)):
                    need.append((seq, ev, ck))
        need.sort(key=lambda x: -x[0])
        for seq, ev, ck in need:
            if clock[e].get(ev[0], 0) >= ev[1]:
                continue
            queue[e].wait_ge(T.sem[ev[0]], ev[1])
            clock[e][ev[0]] = ev[1]
            for k2, n2 in ck.items():
                if clock[e].get(k2, 0) < n2:
                    clock[e][k2] = n2
        return acc

    def note(e, acc, ev, ck):
        seqno[0] += 1
        for name, m, w in acc:
            old = past.get(name, [])
            if w:
                old = [o for o in old if o[0] & ~m]
            past[name] = old + [(m, w, e, ev, ck, seqno[0])]

    def op(e, call, outs, ins):
        acc = order(e, outs, ins)
        done[e] += 1
        call().then_inc(T.sem[csem[e]], 1)
        note(e, acc, (csem[e], done[e]), dict(clock[e]))

    def dma(e, out, in_, outs, ins):
        acc = order(e, outs, ins)
        s = "d%d" % len(dmas)
        dmas.append(s)
        queue[e].dma_start(out, in_).then_inc(T.sem[s], 16)
        note("dma", acc, (s, 16), dict(clock[e]))

    def sc(x):
        return x[0] if isinstance(x, tuple) else x

    def aps(*xs):
        return [x for x in xs if isinstance(x, tuple)]

    def ms(o, c):
        op("v", lambda: g.vector.memset(o[0], c), [o], [])

    def cp(o, i):
        op("v", lambda: g.vector.tensor_copy(o[0], i[0]), [o], [i])

    def tt(o, a, b, f):
        op("v", lambda: g.vector.tensor_tensor(o[0], a[0], b[0], f), [o], [a, b])

    def ts(o, a, s1, f1, s2=None, f2=None):
        if f2 is None:
            op("v", lambda: g.vector.tensor_scalar(o[0], a[0], sc(s1), None, f1), [o], aps(a, s1))
        else:
            op("v", lambda: g.vector.tensor_scalar(o[0], a[0], sc(s1), sc(s2), f1, f2), [o], aps(a, s1, s2))

    def scan(o, a, b, init, f0, f1):
        op("v", lambda: g.vector.tensor_tensor_scan(o[0], a[0], b[0], sc(init), f0, f1), [o], aps(a, b, init))

    def red(o, a, f):
        op("v", lambda: g.vector.tensor_reduce(o[0], a[0], AxisListType.X, f), [o], [a])

    def tr(o, a):
        op("v", lambda: g.vector.transpose(o[0], a[0]), [o], [a])

    def quant(q, s, a):
        op("v", lambda: g.vector.quantize_mx(q[0], s[0], a[0]), [q, s], [a])

    def act(o, a, f, bias=None, scale=None, acc=None):
        kw = {}
        if bias is not None:
            kw["bias"] = sc(bias)
        if scale is not None:
            kw["scale"] = sc(scale)
        if acc is not None:
            kw["accum_out"] = acc[0]
        op("a", lambda: g.scalar.activation(o[0], a[0], f, **kw), aps(o, acc), aps(a, bias, scale))

    def mm(o, wq, ws, xq, xs):
        op("t", lambda: g.tensor.matmul_mx(o[0], wq[0], ws[0], xq[0], xs[0], True, True), [o], [wq, ws, xq, xs])

    def iota(o, pattern, base, cm, small=True):
        if small:
            op("g", lambda: g.iota(o[0], pattern, base, cm, allow_small_or_imprecise_dtypes=True), [o], [])
        else:
            op("g", lambda: g.iota(o[0], pattern, base, cm), [o], [])

    def direct(t):
        return topo.may_write(core, cores[rank ^ (1 << t)])

    def ship(t, k):
        partner = cores[rank ^ (1 << t)]
        src = (V("xq"), V("xs"), V("ol0", 0, 6))[k]
        c = "qsl"[k]
        if direct(t):
            land, dst, sem = T["l" + c + str(t)][:], partner, "a" + c + str(t)
        else:
            land, dst, sem = T["r" + c][:], helpers(topo, core, partner)[min(k, 1)], "h" + c
        eng = topo.engines(core, dst)
        acc = order("g", [], [src])
        rid, pid = topo.addr(dst, core)
        g.remote_dma(land.bitcast(dt.uint8) if k == 0 else land, src[0].bitcast(dt.uint8) if k == 0 else src[0],
                     T.sem[sem], T.sem["s" + c + str(t)], pid, rid, bits(eng))
        sent.append(("s" + c + str(t), len(eng)))
        note("far", acc, sent[-1], dict(clock["g"]))
        note("far", [V("l" + c + str(t))[1:] + (True,)], ("a" + c + str(t), counts(topo, cores, rank, t)[k]), {})

    def fill(o, c, n):
        act(o, V("src", 0, n), F.Identity, bias=c, scale=0.0)

    XB = (V("xq", CA), V("xs", CA))
    XA = (V("xq", 0, CA), V("xs", 0, CA))
    US = (V("u2q", 0, 128), V("u2s", 0, 128))
    UK = (V("u2q", 128), V("u2s", 128))
    nB = C - CA
    hot = lambda lo, hi: V("hot", lo, hi)

    def pick_u(k):
        o, l = V("u2q", 128 * k, 128 * k + 128), V("pl", 8 * k, 8 * k + 8)
        op("v", lambda: g.vector.tensor_copy(o[0].bitcast(dt.uint32), T.uq[:].bitcast(dt.uint32).indirect(l[0])), [o], [V("uq"), l])
        act(V("u2s", 128 * k, 128 * k + 128), IND(V("us"), l), F.Copy)

    def quant_xb():
        quant(XB[0], XB[1], V("X", 4 * CA))

    def quant_xa():
        quant(XA[0], XA[1], V("X", 0, 4 * CA))

    def scan_mb(k):
        if k == 0:
            scan(V("M", CA, C), V("s4", CA, C), P(4, 0, nB), -BIG, A.min, A.max)
        elif k == 1:
            tt(V("Mn", 0, 56), V("M", CA + 3, C, 4), hot(0, 56), A.mult)
        else:
            scan(V("pb"), V("s16", 0, 64), V("Mn"), 0.0, A.mult, A.add)

    def plane(b):
        act(V("Xp", C * (2 * b + 1), C * (2 * b + 2)), V("X", b, 4 * C, 4), F.Copy)

    def mirror(b):
        o, i = back("Xp", 2 * C * b + 1, 2 * C * b + C), V("X", 4 + b, 4 * C, 4)
        op("g", lambda: g.affine_select(o[0], i[0], [[0, C - 1]], A.is_ge, 0.0, 0, 0), [o], [i])

    def marks(t):
        iota(V("mw", 2 * RW * t, 2 * RW * (t + 1)), [[0, 2 * RW]], 1, 0)

    def unpack(t):
        for b in range(4):
            mm(P(4 + b, 0, C), V("eq", 128 * b, 128 * b + 128), V("es", 128 * b, 128 * b + 128), V("lq%d" % t), V("ls%d" % t))

    def unpacked(b):
        act(V("Dp", C * (2 * b + 1), C * (2 * b + 2)), P(4 + b, 0, C), F.Copy)
        act(back("Dp", 2 * C * b + 1, 2 * C * b + C), P(4 + b, 1, C), F.Copy)

    def turn(k, h):
        tr(V("tw", 256 * k + 128 * h, 256 * k + 128 * h + NEW[k]), V("row", LO[k] + 16 * h, LO[k] + 16 * h + NEW[k]))

    def listed(k):
        ts(V("ol%d" % k), IND(V("tw", 256 * k, 256 * k + 256), col("wl", 0)), float(C), A.add)

    def sort(t, spare):
        def gap():
            if spare:
                spare.pop(0)()

        Mv = V("M", 3, C, 4)
        tt(V("Mm", 1, CA), P(6, 1, CA), V("h4", 1, CA), A.add)
        scan(V("M", 1, CA), V("s4", 1, CA), P(6, 1, CA), BIG, A.min, A.max)
        act(V("srow", 1, CA), P(7, 1, CA), F.Copy)
        if t == 0:
            scan_mb(1)
        scan(V("p1"), V("s64"), V("Mm"), -BIG, A.min, A.max)
        if t == 0:
            scan_mb(2)
        for m in (2, 3, 0, 1) if t else (0, 1, 2, 3):
            ts(V("c1", NB * m, NB * m + NB), Mv, col("p1", 64 * m + 63) if m < 2 else col("pb", 16 * m - 17), A.is_lt)
        for m in (4, 5):
            act(V("sa", 128 * (m - 4), 128 * (m - 4) + NB), Mv, F.Sign, bias=col("pb", 16 * m - 17), scale=-1.0)
        for m in (4, 5):
            act(V("sj", 128 * (m - 4), 128 * (m - 4) + NB), V("sa", 128 * (m - 4), 128 * (m - 4) + NB), F.Relu, acc=col("na", m))
        act(V("srow", CA, C), P(4, 0, nB), F.Copy)
        plane(0)
        plane(1)
        halves = (1, 0) if t else (0, 1)
        for h in halves:
            scan(V("n1", 2 * NB * h, 2 * NB * (h + 1)), V("s88"), V("c1", 2 * NB * h, 2 * NB * (h + 1)), 0.0, A.min, A.add)
        for h in (halves[0], 2, halves[1]):
            cp(V("o1", 2 * h, 2 * h + 2), V("n1", (2 * h + 1) * NB - 1, (2 * h + 2) * NB, NB) if h < 2 else V("na", 4, 6))
        for lo, hi in ((2, 6), (0, 2)) if t else ((0, 2), (2, 6)):
            cp(V("f1", 16 * lo, 16 * hi), IND(V("tf"), V("o1", lo, hi)))
        tt(V("v1"), IND(V("tb"), V("o1", 0, 6)), V("M", 3, 384, 4), A.min)
        scan(V("q1", 0, NB), V("f1", 0, NB), V("f1", 0, NB), 0.0, A.add, A.max)
        for m in range(2):
            act(V("sj", 128 * m, 128 * m + NB), V("q1", 0, NB), F.Sign, bias=col("rb", m), acc=col("nb", m))
        scan(back("srow", C, 448), V("v1"), V("v1"), -BIG, A.max, A.max)
        gap()
        for m in range(2):
            ts(V("oc4", 4 * m, 4 * m + 4), V("b4"), col("nb", m), A.subtract, 2.0, A.mult)
        for h in range(2):
            l = V("oc4", 4 * h, 4 * h + 4)
            act(V("cand", 64 * h, 64 * h + 64), IND(V("srow"), l), F.Copy)
            tt(V("cm", 64 * h, 64 * h + 64), IND(V("srow"), l), hot(0, 64), A.mult)
        for h in range(2):
            scan(V("p2", 64 * h, 64 * h + 64), V("s16", 0, 64), V("cm", 64 * h, 64 * h + 64), 0.0, A.mult, A.add)
        for m in range(3):
            act(V("sa", 128 * m, 128 * m + 128), V("cand"), F.Sign, bias=col("p2", 16 * m + 15), scale=-1.0)
        for m in range(3):
            act(V("sj", 128 * m, 128 * m + 128), V("sa", 128 * m, 128 * m + 128), F.Relu, scale=-1.0, acc=col("nc", m))
        for m in range(3, 8):
            ts(V("c2", 128 * m - 384, 128 * m - 256), V("cand"), col("p2", 16 * m + 15), A.is_gt)
        act(V("krow", CA), P(5, 0, nB), F.Copy)
        act(V("ksh", CA + 1, C + 1), P(5, 0, nB), F.Copy)
        act(V("krow", 0, CA), P(0, 0, CA), F.Copy)
        act(V("ksh", 1, CA + 1), P(0, 0, CA), F.Copy)
        act(col("kl", 32), col("krow", C - 1), F.Copy)
        plane(2)
        scan(V("n2", 0, 384), V("s128"), V("c2", 0, 384), 0.0, A.mult, A.add)
        scan(V("n2", 384), V("s128", 0, 256), V("c2", 384), 0.0, A.mult, A.add)
        cp(V("o2", 0, 3), V("nc", 0, 3))
        cp(V("o2", 3, 6), V("n2", 127, 384, 128))
        cp(V("o2", 6, 8), V("n2", 511, 640, 128))
        tt(V("v2", 0, 96), IND(V("tc"), V("o2", 0, 6)), V("cand", 0, 96), A.max)
        tt(V("v2", 96), IND(V("tc"), V("o2", 6, 8)), V("cand", 96), A.max)
        gap()
        red(col("t1", 0), V("v2"), A.min)
        gap()
        ts(V("gt"), V("srow", 0, C), col("t1", 0), A.is_gt, -1.0, A.mult)
        act(V("sg", MID), V("srow", MID, C), F.Sign, bias=col("t1", 0), scale=-1.0)
        act(V("ge", MID), V("sg", MID), F.Sign, bias=1.0, scale=-1.0)
        plane(3)
        ts(V("ge", 0, MID), V("srow", 0, MID), col("t1", 0), A.is_ge)
        scan(back("pg", 1, C), back("gt", 1, C), back("gt", 1, C), 32.0, A.add, A.max)
        gap()
        scan(V("pp"), V("ge"), V("pg", 1, C + 1), 0.0, A.add, A.min)
        gap()
        act(V("sg", 0, C - 16), V("pp", 0, C - 16), F.Sign, bias=col("rb", 0), acc=col("nd", 0))
        ts(V("le", 16), V("pp", 16), col("rb", 2), A.is_le)
        gap()
        scan(V("lc", 16), V("le", 16), V("zt", 16), float(16 - MID), A.add, A.add)
        ts(col("o3", 0), col("nd", 0), -0.5, A.mult, float(C - 16) / 2, A.add)
        ts(col("o3", 2), col("lc", C - 1), float(MID), A.add)
        L = (col("o3", 0), col("o3", 2))
        for n, w, h in (("eb", "iw", 0), ("kb", "krow", 0), ("eb", "iw", 1), ("kb", "krow", 1), ("kl", "ksh", 0), ("kl", "ksh", 1)):
            act(V(n, 16 * h, 16 * h + 16), IND(V(w), L[h]), F.Copy)
        for h in range(2):
            tt(V("km", 16 * h, 16 * h + 16), IND(V("krow"), L[h]), hot(0, 16), A.mult)
            tt(V("ke", 16 * h, 16 * h + 16), IND(V("krow"), L[h]), V("tri", 16 * h, 16 * h + 16), A.add)
        red(col("p3", 0), V("km", 0, 16), A.add)
        tt(V("wt", 0, 15), V("eb", 1, 16), V("eb", 0, 15), A.subtract)
        red(col("p3", 1), V("km", 16), A.add)
        tt(V("wt", 16, 48), V("eb", 1, 33), V("eb", 0, 32), A.subtract)
        tt(V("wt", 48), V("eb", 16, 32), V("eb", 17, 33), A.subtract)
        ts(V("c3", 0, 16), V("ke", 0, 16), col("p3", 0), A.is_equal)
        ts(V("c3", 16, 48), V("kb"), col("p3", 0), A.is_gt)
        ts(V("c3", 48, 80), V("kb"), col("p3", 1), A.is_ge)
        ts(V("c3", 80), V("ke", 16), col("p3", 1), A.is_equal)
        for h in range(2):
            act(V("el", 16 * h, 16 * h + 16), IND(V("iw"), L[h]), F.Identity, bias=-1.0)
        unpack(t)
        for b in range(4):
            unpacked(b)
        tt(V("tn"), V("kb"), V("kl", 1, 33), A.is_lt)
        for h in range(2):
            tt(V("m3", 48 * h, 48 * h + 48), V("c3", 48 * h, 48 * h + 48), V("wt", 16 * h, 16 * h + 48), A.mult)
        tt(V("hl"), V("eb", 0, 32), V("el", 1, 33), A.add)
        for h in range(2):
            red(col("n3", h), V("m3", 48 * h, 48 * h + 48), A.add)
        tt(V("t2"), V("hl"), V("tn"), A.mult)
        gap()
        ts(V("o4"), V("n3"), col("cf", 3), A.add)
        tt(V("ff"), V("eb", 0, 32), V("t2"), A.subtract)
        mw, dw = 2 * RW * t, 2 * RW * t + RW
        cp(IND(V("mw", mw, mw + RW), V("o4")), V("z32"))
        cp(IND(V("mw", dw, dw + RW), V("o4")), V("ff"))
        while spare:
            gap()
        scan(V("row"), V("mw", mw, mw + RW), V("mw", dw, dw + RW), 0.0, A.mult, A.add)
        a, b = (1, 0) if direct(t) else (0, 1)
        for k in (a, b):
            turn(k, 0)
            turn(k, 1)
        listed(a)
        turn(2, 0)
        listed(b)
        turn(2, 1)
        ship(t, 2)

    LO, NEW, BANK = (0, K, K + 128), (K, 128, 128), (0, 0, 4)

    def pick(e, t, k, b):
        o = V("E", 4 * LO[k] + b, 4 * (LO[k] + NEW[k]), 4)
        src = IND(V("Xp" if k else "Dp", 2 * C * b, 2 * C * (b + 1)), V("ol%d" % k, 0, 8) if k else V("ll%d" % t))
        if e == "v":
            cp(o, src)
        else:
            act(o, src, F.Copy)

    def layer(k):
        q, s = V("hq", 128 * k, 128 * k + 128), V("hs", 128 * k, 128 * k + 128)
        quant(q, s, V("E", 4 * LO[k], 4 * LO[k] + 512))
        for b in range(4):
            mm(P(BANK[k] + b, 0, 128), V("wq", 128 * b, 128 * b + 128), V("wp", 128 * b, 128 * b + 128), q, s)

    def rl(k, b):
        return V("Rl", 512 * k + 128 * b, 512 * k + 128 * b + NEW[k])

    def relu(k, *bs):
        for b in bs:
            act(rl(k, b), P(BANK[k] + b, 0, NEW[k]), F.Relu, scale=0.015625)

    def add(k, *bs):
        for b in bs:
            lo, hi = 4 * LO[k] + b, 4 * (LO[k] + NEW[k])
            tt(V("X", lo, hi, 4), V("E", lo, hi, 4), rl(k, b), A.add)

    def swap(t):
        last = t == R - 1
        pick("a", t, 1, 0)
        pick("a", t, 1, 1)
        pick("v", t, 1, 2)
        listed(2)
        if not last:
            marks(t + 1)
        pick("v", t, 1, 3)
        pick("a", t, 2, 0)
        pick("a", t, 2, 1)
        pick("v", t, 2, 2)
        layer(1)
        pick("v", t, 2, 3)
        layer(2)
        relu(1, 0, 1, 2, 3)
        add(1, 0)

        def places():
            if last:
                act(V("ob"), V("row"), F.Abs)
                for h in range(2):
                    dma("s", T.ol[h:8:2, :], T.ob[16 * h:128:32, 16 * h:16 * h + C], [], [V("ob")])

        def scores_b():
            for k in (1, 2):
                quant(V("xq", LO[k], LO[k] + 128), V("xs", LO[k], LO[k] + 128), V("X", 4 * LO[k], 4 * LO[k] + 512))
            if last:
                mm(P(4, 0, nB), V("vq"), V("vs"), XB[0], XB[1])
                dma("s", T.oc[:, 4 * CA:4 * C], T.xq[:, CA:C].bitcast(dt.uint8), [], [XB[0]])
            else:
                mm(P(4, 0, nB), US[0], US[1], XB[0], XB[1])
                mm(P(5, 0, nB), UK[0], UK[1], XB[0], XB[1])

        if direct(t):
            relu(2, 0, 1)
            pick("a", t, 0, 0)
            pick("a", t, 0, 1)
            relu(2, 2, 3)
            pick("a", t, 0, 2)
            places()
            add(1, 1, 2, 3)
            add(2, 0)
            pick("v", t, 0, 3)
            add(2, 1)
            layer(0)
            relu(0, 0, 1, 2, 3)
            add(2, 2, 3)
            scores_b()
            add(0, 0, 1, 2, 3)
        else:
            relu(2, 0, 1, 2, 3)
            places()
            add(1, 1, 2, 3)
            add(2, 0, 1)
            for b in range(4):
                pick("av"[b // 2], t, 0, b)
            layer(0)
            relu(0, 0, 1, 2, 3)
            add(2, 2, 3)
            scores_b()
            add(0, 0, 1, 2, 3)
        if last:
            act(V("yb", CA), P(4, 0, nB), F.Copy)
            dma("s", T.y[:, CA:C], T.yb[:, CA:C], [], [V("yb", CA)])
            quant_xa()
            mm(P(6, 0, CA), V("vq"), V("vs"), XA[0], XA[1])
            dma("s", T.oc[:, 0:4 * CA], T.xq[:, 0:CA].bitcast(dt.uint8), [], [XA[0]])
            for k in range(4):
                dma("as"[k // 2], T.osc[4 * k:4 * k + 4, :], T.xs[32 * k:32 * k + 4, :], [], [V("xs")])
            cp(V("yb", 0, CA), P(6, 0, CA))
            dma("a", T.y[:, 0:CA], T.yb[:, 0:CA], [], [V("yb", 0, CA)])
        else:
            scan_mb(0)
            quant_xa()
            mm(P(6, 0, CA), US[0], US[1], XA[0], XA[1])
            mm(P(7, 0, CA), US[0], US[1], XA[0], XA[1])
            mm(P(0, 0, CA), UK[0], UK[1], XA[0], XA[1])
            ship(t + 1, 0)
            ship(t + 1, 1)
            for b in range(4):
                mirror(b)
            scan_mb(1)
            scan_mb(2)

    dma("s", T.ut[:], T.u[:], [V("ut")], [])
    dma("s", T.X[:, 4 * CA:4 * C], T.x[:, 4 * CA:4 * C], [V("X", 4 * CA)], [])
    dma("s", T.X[:, 0:4 * CA], T.x[:, 0:4 * CA], [V("X", 0, 4 * CA)], [])
    iota(V("pi"), [[1, 2], [16, 8]], 0, 0)
    iota(col("ci", 0), [[0, 1]], 0, 1, False)
    iota(V("j16"), [[0, 8], [1, 16]], 0, 0)
    iota(V("j4"), [[0, 2], [1, 16], [0, 4]], 0, 0)
    iota(V("s88"), [[0, 2], [256, NB]], 0, 0)
    ms(V("src"), 0.0)
    ms(V("one"), 1.0)
    cp(V("pl"), V("pi"))
    for c, m in enumerate((15, 1, 6, 16)):
        ts(col("ci", c + 1), col("ci", 0), m, A.bitwise_and)
    for o, x in ((V("tf", 0, 57), 0.0), (V("tf", 57), 1.0)):
        ms(o, x)
    cp(V("cf", 0, 4), V("ci", 1, 5))
    for o, x in ((V("tb", 0, 57), BIG), (V("tb", 57), -BIG)):
        ms(o, x)
    ts(V("hot"), V("j16"), col("cf", 0), A.is_equal)
    ts(V("h4"), V("j4"), col("cf", 0), A.not_equal, -BIG, A.mult)

    def unit(h):
        o = V("et%d" % h)
        op("g", lambda: g.affine_select(o[0], T.one[:], [[1, 514]], A.is_equal, 0.0, -2 - h, -4), [o], [V("one")])

    def quant_e(b):
        lo = 2 - b // 2 * 2
        quant(V("eq", 128 * b, 128 * b + 128), V("es", 128 * b, 128 * b + 128), V("et%d" % (b % 2), lo, lo + 512))

    unit(0)
    for b in (1, 2, 3):
        fill(V("s4", b, C, 4), BIG, NB)
    fill(V("s4", 0, C, 4), -BIG, NB)
    for o, x, n in ((V("s64"), BIG, 128), (V("M", C), -BIG, 32), (col("srow", 0), BIG, 1), (V("tc", 0, 32), -BIG, 32),
                    (V("s64", 0, 128, 64), -BIG, 2), (V("tc", 32), BIG, 96), (col("ksh", 0), 0.0, 1), (V("ksh", C + 1), 0.0, 7),
                    (V("pg", C), 32.0, 8), (col("eb", 32), float(C), 1), (col("el", 32), float(C - 1), 1), (V("z32"), 0.0, 32),
                    (col("wt", 15), 0.0, 1)):
        fill(o, x, n)
    act(V("s16"), V("j16"), F.Sign)
    act(col("Mm", 0), col("hot", 0), F.Identity, bias=-BIG, scale=2 * BIG)
    act(V("Mn", 56), hot(8, 16), F.Identity, scale=-BIG)
    quant(V("uq"), V("us"), V("ut"))
    ms(V("s128"), 1.0)
    pick_u(0)
    quant_xb()
    mm(P(4, 0, nB), US[0], US[1], XB[0], XB[1])
    quant_xa()
    mm(P(6, 0, CA), US[0], US[1], XA[0], XA[1])
    mm(P(7, 0, CA), US[0], US[1], XA[0], XA[1])
    ship(0, 0)
    ship(0, 1)
    pick_u(1)
    mm(P(5, 0, nB), UK[0], UK[1], XB[0], XB[1])
    mm(P(0, 0, CA), UK[0], UK[1], XA[0], XA[1])
    act(V("b4"), V("j16", 0, 4), F.Identity, bias=float(NB), scale=0.5)
    for c, x, s in ((0, -0.5, -1.0), (1, -16.5, -1.0), (2, 16.0, 1.0)):
        act(col("rb", c), col("cf", 0), F.Identity, bias=x, scale=s)
    for o, n in ((V("tw", K, 128), 32), (V("tw", 128 + K, 256), 32), (V("Xp", 0, 8 * C, 2 * C), 4), (V("Dp", 0, 8 * C, 2 * C), 4)):
        fill(o, 0.0, n)
    dma("s", T.wq[:].bitcast(dt.uint8), T.wc[:], [V("wq")], [col("X", 0), col("X", 4 * CA)])
    dma("s", T.wp[:], T.ws[:], [V("wp")], [])
    dma("s", T.vt[:], T.v[:], [V("vt")], [])
    unit(1)
    iota(V("iw"), [[1, 360]], 0, 0)
    marks(0)
    for b in range(4):
        mirror(b)
    ms(V("s128", 0, 384, 128), 0.0)
    scan_mb(0)

    def small():
        ms(V("zt"), 0.0)
        ts(V("tri", 0, 16), V("j16", 0, 16), col("cf", 0), A.is_ge, -BIG, A.mult)
        ts(V("tri", 16), V("j16", 0, 16), col("cf", 0), A.is_lt, -BIG, A.mult)

    first = [small, lambda: ts(col("cf", 4), col("cf", 1), 128.0, A.mult, col("cf", 3), A.add)]
    first += [lambda b=b: quant_e(b) for b in range(4)]
    first += [lambda: ts(col("wl", 0), col("cf", 2), 16.0, A.mult, col("cf", 4), A.add)]
    for t in range(R):
        sort(t, first if t == 0 else [lambda: quant(V("vq"), V("vs"), V("vt"))] if t == 1 else [])
        swap(t)
    for s, n in sent:
        g.wait_ge(T.sem[s], n)
    for e in csem:
        g.wait_ge(T.sem[csem[e]], done[e])
    for s in dmas:
        g.wait_ge(T.sem[s], 16)
